import numpy as np
import ml_dtypes


def mxq(x, axis, fmt="e4m3"):
    dtype, down = {"e4m3": (ml_dtypes.float8_e4m3fn, 7), "e5m2": (ml_dtypes.float8_e5m2, 14)}[fmt]
    v = np.moveaxis(np.asarray(x, np.float32).astype(ml_dtypes.bfloat16).astype(np.float64), axis, -1)
    blocks = v.reshape(v.shape[:-1] + (-1, 32))
    amax = np.abs(blocks).max(-1, keepdims=True)
    byte = np.maximum(np.where(amax > 0, np.frexp(amax)[1] - 1 + 127, 0) - down, 1)
    scale = np.exp2(byte - 127.0)
    codes = (blocks / scale).astype(np.float32).astype(dtype).astype(np.float64)
    return np.moveaxis((codes * scale).reshape(v.shape), -1, axis)


WIDE = False


def mx_kscale(k):
    if not WIDE:
        return np.ones(k)
    levels = np.array([10, -10, 5, -5, 0])
    if k % 512:
        return np.exp2(np.random.permutation(np.resize(levels, k // 32))).repeat(32)
    a = np.empty((k // 512, 16))
    for p in range(k // 512):
        a[p, :8] = np.random.permutation(np.resize(levels, 8))
        for g in range(8):
            far = levels[np.abs(levels - a[p, g]) >= 10]
            a[p, g + 8] = far[np.random.randint(len(far))]
    return np.exp2(a.ravel()).repeat(32)


def f64(x):
    return np.asarray(x).astype(np.float64)


def striped(idx):
    return np.tile(idx.reshape(-1, 16).T, (8, 1)).astype(np.uint16)


def unstriped(offs):
    return offs[:16].T.reshape(-1).astype(np.int64)


def pack_weight(w):
    k, n = w.shape
    w = f64(np.asarray(w, np.float32).astype(ml_dtypes.bfloat16)).reshape(k // 32, 32, n)
    amax = np.abs(w).max(1)
    byte = np.clip(np.where(amax > 0, np.frexp(amax)[1] - 1 + 127 - 7, 1), 1, 254)
    scaled = (w * np.exp2(127.0 - byte)[:, None, :]).reshape(k, n).astype(np.float32)
    words = np.ascontiguousarray(scaled.reshape(k // 512, 128, 4, n).transpose(0, 1, 3, 2)).astype(ml_dtypes.float8_e4m3fn).view(np.uint8)
    return words, np.ascontiguousarray(byte.astype(np.uint8).reshape(k // 512, 16, n))


def unpack_weight(words, scales):
    g, p, n, _ = words.shape
    vals = np.ascontiguousarray(words).view(ml_dtypes.float8_e4m3fn).astype(np.float64) * np.repeat(np.exp2(scales.astype(np.float64) - 127.0), 8, axis=1)[..., None]
    return vals.transpose(0, 1, 3, 2).reshape(g * 512, n)


K, T, S, V, N = 512, 4096, 1024, 512, 128
P = 2 ** 7


def setup_inputs():
    n = np.random.standard_normal
    s = mx_kscale(K)[:, None]
    packed_xT = pack_weight(n((K, T)) * s)
    return {
        "x_words": packed_xT[0],
        "x_scales": packed_xT[1],
        "w1": (n((K, N)) / np.sqrt(K) / s).astype(np.float32),
        "frac": np.tile(np.random.uniform(0.05, 0.95, V), (P, 1)).astype(np.float32),
        "offs": striped(np.random.permutation(T)[:S]),
        "left": striped(np.random.permutation(S)[:V]),
        "right": striped(np.random.permutation(S)[:V]),
    }


def reference(x_words, x_scales, w1, frac, offs, left, right):
    xq = unpack_weight(x_words, x_scales)[:, unstriped(offs)]
    y = mxq(f64(w1), 0, "e4m3").T @ xq
    l = y[:, unstriped(left)]
    return l + (y[:, unstriped(right)] - l) * f64(frac)[:1]

@@ -1,0 +1,105 @@
+from contextlib import ExitStack
+
+import concourse.mybir as mybir
+
+K, T, S, V, M = 512, 4096, 1024, 512, 128
+FLOPS = 2 * K * M * S
+
+F32 = mybir.dt.float32
+BF16 = mybir.dt.bfloat16
+I32 = mybir.dt.int32
+U32 = mybir.dt.uint32
+U16 = mybir.dt.uint16
+U8 = mybir.dt.uint8
+FP8X4 = mybir.dt.float8_e4m3fn_x4
+MULT = mybir.AluOpType.mult
+ADD = mybir.AluOpType.add
+
+P = 128
+PACK = 4
+LANES = 16
+
+
+def tile_picked_lerp_none_p_kernel(
+    tc, x_words, x_scales, w1, frac, offs, left, right, out
+):
+    nc = tc.nc
+    with ExitStack() as ctx:
+        keep = ctx.enter_context(tc.tile_pool(name="keep", bufs=1))
+        psum = ctx.enter_context(tc.psum_pool(name="psum", bufs=1))
+
+        offs_sb = keep.tile([P, S // LANES], U16, name="offs_sb")
+        left_sb = keep.tile([P, V // LANES], U16, name="left_sb")
+        right_sb = keep.tile([P, V // LANES], U16, name="right_sb")
+        w_raw = keep.tile([P, PACK, M], F32, name="w_raw")
+        words = keep.tile([P, T], I32, name="words", align_bytes=64)
+        frac_sb = keep.tile([P, V], F32, name="frac_sb")
+        scale_rows = keep.tile([P, T], U8, name="scale_rows", tag="shared", align_bytes=64)
+
+        nc.vector.memset(scale_rows[:].bitcast(I32), 0)
+        nc.sync.dma_start(out=w_raw[:], in_=w1.rearrange("(p j) m -> p j m", j=PACK))
+        nc.sync.dma_start(offs_sb[:], offs)
+        nc.sync.dma_start(left_sb[:], left)
+        nc.sync.dma_start(out=words[:], in_=x_words[0].rearrange("p n t -> p (n t)").bitcast(I32))
+        nc.sync.dma_start(right_sb[:], right)
+        nc.sync.dma_start(out=frac_sb[:], in_=frac)
+        nc.scalar.dma_start(out=scale_rows[32:96:4, :].bitcast(I32), in_=x_scales[0].bitcast(I32))
+
+        x_plane = keep.tile([P, S], U8, name="x_plane", align_bytes=64)
+        nc.vector.memset(x_plane[:].bitcast(I32), 0)
+
+        picked_scales = keep.tile([P, S], U8, name="picked_scales", align_bytes=64)
+        nc.vector.tensor_copy(picked_scales[:], scale_rows[:].indirect(offs_sb[:]))
+        for q in range(4):
+            nc.scalar.dma_start(
+                out=x_plane[32 * q : 32 * q + 4, :].bitcast(I32),
+                in_=picked_scales[32 + 16 * q : 48 + 16 * q : 4, :].bitcast(I32),
+            )
+
+        w_bf = keep.tile([P, M, PACK], BF16, name="w_bf", align_bytes=64)
+        nc.vector.tensor_copy(out=w_bf[:], in_=w_raw[:].rearrange("p j m -> p m j"))
+        w_codes = keep.tile([P, M], U32, name="w_codes", align_bytes=64)
+        w_plane = keep.tile([P, M], U8, name="w_plane", align_bytes=64)
+        nc.vector.quantize_mx(
+            out=w_codes[:].bitcast(FP8X4), scales=w_plane[:], in_=w_bf[:].rearrange("p m j -> p (m j)")
+        )
+
+        picked = keep.tile([P, S], U32, name="picked", tag="shared", align_bytes=64)
+        y = keep.tile([P, S], F32, name="y", align_bytes=64)
+        rest = keep.tile([P, V], F32, name="rest")
+
+        def gather_words(a, b):
+            nc.vector.tensor_copy(picked[:, a:b], words[:].bitcast(U32).indirect(offs_sb[:, a // LANES : b // LANES]))
+
+        def project(a, b):
+            acc = psum.tile([M, b - a], F32, name="acc%d" % a)
+            nc.tensor.matmul_mx(
+                out=acc[:],
+                lhsT=w_codes[:].bitcast(FP8X4),
+                lhsT_scale=w_plane[:],
+                rhs=picked[:, a:b].bitcast(FP8X4),
+                rhs_scale=x_plane[:, a:b],
+                start=True,
+                stop=True,
+            )
+            return acc
+
+        gather_words(0, 512)
+        nc.scalar.copy(y[:, 0:512], project(0, 512)[:])
+        gather_words(512, 1024)
+        nc.scalar.copy(y[:, 512:768], project(512, 768)[:])
+        nc.vector.tensor_scalar(rest[:], frac_sb[:], -1.0, 1.0, MULT, ADD)
+        nc.vector.tensor_copy(y[:, 768:1024], project(768, 1024)[:])
+
+        from_right = keep.tile([P, V], F32, name="from_right")
+        from_left = keep.tile([P, V], F32, name="from_left")
+        result = keep.tile([P, V], F32, name="result")
+        nc.vector.tensor_tensor(from_right[:], y[:].indirect(right_sb[:]), frac_sb[:], MULT)
+        halves = ((0, 256), (256, 512))
+        for a, b in halves:
+            nc.vector.tensor_tensor(
+                from_left[:, a:b], y[:].indirect(left_sb[:, a // LANES : b // LANES]), rest[:, a:b], MULT
+            )
+        for (a, b), queue in zip(halves, (nc.sync, nc.scalar)):
+            nc.vector.tensor_tensor(result[:, a:b], from_left[:, a:b], from_right[:, a:b], ADD)
+            queue.dma_start(out=out[:, a:b], in_=result[:, a:b])

@@ -33,17 +33,15 @@ def tile_picked_lerp_none_p_kernel(
         right_sb = keep.tile([P, V // LANES], U16, name="right_sb")
         w_raw = keep.tile([P, PACK, M], F32, name="w_raw")
         words = keep.tile([P, T], I32, name="words", align_bytes=64)
-        frac_sb = keep.tile([P, V], F32, name="frac_sb")
         scale_rows = keep.tile([P, T], U8, name="scale_rows", tag="shared", align_bytes=64)
 
         nc.vector.memset(scale_rows[:].bitcast(I32), 0)
         nc.sync.dma_start(out=w_raw[:], in_=w1.rearrange("(p j) m -> p j m", j=PACK))
         nc.sync.dma_start(offs_sb[:], offs)
         nc.sync.dma_start(left_sb[:], left)
-        nc.sync.dma_start(out=words[:], in_=x_words[0].rearrange("p n t -> p (n t)").bitcast(I32))
         nc.sync.dma_start(right_sb[:], right)
-        nc.sync.dma_start(out=frac_sb[:], in_=frac)
-        nc.scalar.dma_start(out=scale_rows[32:96:4, :].bitcast(I32), in_=x_scales[0].bitcast(I32))
+        nc.sync.dma_start(out=scale_rows[32:96:4, :].bitcast(I32), in_=x_scales[0].bitcast(I32))
+        nc.sync.dma_start(out=words[:], in_=x_words[0].rearrange("p n t -> p (n t)").bitcast(I32))
 
         x_plane = keep.tile([P, S], U8, name="x_plane", align_bytes=64)
         nc.vector.memset(x_plane[:].bitcast(I32), 0)
@@ -55,6 +53,8 @@ def tile_picked_lerp_none_p_kernel(
                 out=x_plane[32 * q : 32 * q + 4, :].bitcast(I32),
                 in_=picked_scales[32 + 16 * q : 48 + 16 * q : 4, :].bitcast(I32),
             )
+        frac_sb = keep.tile([P, V], F32, name="frac_sb", tag="shared", align_bytes=64)
+        nc.sync.dma_start(out=frac_sb[:], in_=frac)
 
         w_bf = keep.tile([P, M, PACK], BF16, name="w_bf", align_bytes=64)
         nc.vector.tensor_copy(out=w_bf[:], in_=w_raw[:].rearrange("p j m -> p m j"))
@@ -64,7 +64,7 @@ def tile_picked_lerp_none_p_kernel(
             out=w_codes[:].bitcast(FP8X4), scales=w_plane[:], in_=w_bf[:].rearrange("p m j -> p (m j)")
         )
 
-        picked = keep.tile([P, S], U32, name="picked", tag="shared", align_bytes=64)
+        picked = keep.tile([P, S], U32, name="picked", align_bytes=64)
         y = keep.tile([P, S], F32, name="y", align_bytes=64)
         rest = keep.tile([P, V], F32, name="rest")
 

@@ -18,6 +18,7 @@ ADD = mybir.AluOpType.add
 P = 128
 PACK = 4
 LANES = 16
+HEAD = 512
 
 
 def tile_picked_lerp_none_p_kernel(
@@ -40,8 +41,10 @@ def tile_picked_lerp_none_p_kernel(
         nc.sync.dma_start(offs_sb[:], offs)
         nc.sync.dma_start(left_sb[:], left)
         nc.sync.dma_start(right_sb[:], right)
+        words_hbm = x_words[0].rearrange("p n t -> p (n t)").bitcast(I32)
+        nc.sync.dma_start(out=words[:, :HEAD], in_=words_hbm[:, :HEAD])
         nc.sync.dma_start(out=scale_rows[32:96:4, :].bitcast(I32), in_=x_scales[0].bitcast(I32))
-        nc.sync.dma_start(out=words[:], in_=x_words[0].rearrange("p n t -> p (n t)").bitcast(I32))
+        nc.sync.dma_start(out=words[:, HEAD:], in_=words_hbm[:, HEAD:])
 
         x_plane = keep.tile([P, S], U8, name="x_plane", align_bytes=64)
         nc.vector.memset(x_plane[:].bitcast(I32), 0)
@@ -49,7 +52,7 @@ def tile_picked_lerp_none_p_kernel(
         picked_scales = keep.tile([P, S], U8, name="picked_scales", align_bytes=64)
         nc.vector.tensor_copy(picked_scales[:], scale_rows[:].indirect(offs_sb[:]))
         for q in range(4):
-            nc.scalar.dma_start(
+            (nc.sync, nc.scalar)[q % 2].dma_start(
                 out=x_plane[32 * q : 32 * q + 4, :].bitcast(I32),
                 in_=picked_scales[32 + 16 * q : 48 + 16 * q : 4, :].bitcast(I32),
             )
@@ -57,7 +60,7 @@ def tile_picked_lerp_none_p_kernel(
         nc.sync.dma_start(out=frac_sb[:], in_=frac)
 
         w_bf = keep.tile([P, M, PACK], BF16, name="w_bf", align_bytes=64)
-        nc.vector.tensor_copy(out=w_bf[:], in_=w_raw[:].rearrange("p j m -> p m j"))
+        nc.scalar.copy(w_bf[:], w_raw[:].rearrange("p j m -> p m j"))
         w_codes = keep.tile([P, M], U32, name="w_codes", align_bytes=64)
         w_plane = keep.tile([P, M], U8, name="w_plane", align_bytes=64)
         nc.vector.quantize_mx(
@@ -87,9 +90,10 @@ def tile_picked_lerp_none_p_kernel(
         gather_words(0, 512)
         nc.scalar.copy(y[:, 0:512], project(0, 512)[:])
         gather_words(512, 1024)
-        nc.scalar.copy(y[:, 512:768], project(512, 768)[:])
         nc.vector.tensor_scalar(rest[:], frac_sb[:], -1.0, 1.0, MULT, ADD)
-        nc.vector.tensor_copy(y[:, 768:1024], project(768, 1024)[:])
+        nc.vector.tensor_copy(y[:, 512:768], project(512, 768)[:])
+        nc.scalar.copy(y[:, 768:896], project(768, 896)[:])
+        nc.scalar.copy(y[:, 896:1024], project(896, 1024)[:])
 
         from_right = keep.tile([P, V], F32, name="from_right")
         from_left = keep.tile([P, V], F32, name="from_left")

@@ -18,7 +18,7 @@ ADD = mybir.AluOpType.add
 P = 128
 PACK = 4
 LANES = 16
-HEAD = 512
+HEAD = 384
 
 
 def tile_picked_lerp_none_p_kernel(
@@ -39,12 +39,13 @@ def tile_picked_lerp_none_p_kernel(
         nc.vector.memset(scale_rows[:].bitcast(I32), 0)
         nc.sync.dma_start(out=w_raw[:], in_=w1.rearrange("(p j) m -> p j m", j=PACK))
         nc.sync.dma_start(offs_sb[:], offs)
-        nc.sync.dma_start(left_sb[:], left)
-        nc.sync.dma_start(right_sb[:], right)
         words_hbm = x_words[0].rearrange("p n t -> p (n t)").bitcast(I32)
-        nc.sync.dma_start(out=words[:, :HEAD], in_=words_hbm[:, :HEAD])
+        for a in range(0, 2 * HEAD, HEAD):
+            nc.sync.dma_start(out=words[:, a : a + HEAD], in_=words_hbm[:, a : a + HEAD])
         nc.sync.dma_start(out=scale_rows[32:96:4, :].bitcast(I32), in_=x_scales[0].bitcast(I32))
-        nc.sync.dma_start(out=words[:, HEAD:], in_=words_hbm[:, HEAD:])
+        nc.sync.dma_start(out=words[:, 2 * HEAD :], in_=words_hbm[:, 2 * HEAD :])
+        nc.sync.dma_start(right_sb[:], right)
+        nc.sync.dma_start(left_sb[:], left)
 
         x_plane = keep.tile([P, S], U8, name="x_plane", align_bytes=64)
         nc.vector.memset(x_plane[:].bitcast(I32), 0)
@@ -52,7 +53,7 @@ def tile_picked_lerp_none_p_kernel(
         picked_scales = keep.tile([P, S], U8, name="picked_scales", align_bytes=64)
         nc.vector.tensor_copy(picked_scales[:], scale_rows[:].indirect(offs_sb[:]))
         for q in range(4):
-            (nc.sync, nc.scalar)[q % 2].dma_start(
+            nc.sync.dma_start(
                 out=x_plane[32 * q : 32 * q + 4, :].bitcast(I32),
                 in_=picked_scales[32 + 16 * q : 48 + 16 * q : 4, :].bitcast(I32),
             )
@@ -91,9 +92,8 @@ def tile_picked_lerp_none_p_kernel(
         nc.scalar.copy(y[:, 0:512], project(0, 512)[:])
         gather_words(512, 1024)
         nc.vector.tensor_scalar(rest[:], frac_sb[:], -1.0, 1.0, MULT, ADD)
-        nc.vector.tensor_copy(y[:, 512:768], project(512, 768)[:])
-        nc.scalar.copy(y[:, 768:896], project(768, 896)[:])
-        nc.scalar.copy(y[:, 896:1024], project(896, 1024)[:])
+        for a in range(512, 1024, 128):
+            nc.scalar.copy(y[:, a : a + 128], project(a, a + 128)[:])
 
         from_right = keep.tile([P, V], F32, name="from_right")
         from_left = keep.tile([P, V], F32, name="from_left")

@@ -1,6 +1,7 @@
 from contextlib import ExitStack
 
 import concourse.mybir as mybir
+from concourse.masks import make_identity
 
 K, T, S, V, M = 512, 4096, 1024, 512, 128
 FLOPS = 2 * K * M * S
@@ -14,11 +15,12 @@ U8 = mybir.dt.uint8
 FP8X4 = mybir.dt.float8_e4m3fn_x4
 MULT = mybir.AluOpType.mult
 ADD = mybir.AluOpType.add
+COPY = mybir.ActivationFunctionType.Copy
 
 P = 128
 PACK = 4
 LANES = 16
-HEAD = 384
+HEAD = 448
 
 
 def tile_picked_lerp_none_p_kernel(
@@ -34,14 +36,18 @@ def tile_picked_lerp_none_p_kernel(
         right_sb = keep.tile([P, V // LANES], U16, name="right_sb")
         w_raw = keep.tile([P, PACK, M], F32, name="w_raw")
         words = keep.tile([P, T], I32, name="words", align_bytes=64)
-        scale_rows = keep.tile([P, T], U8, name="scale_rows", tag="shared", align_bytes=64)
+        scale_rows = keep.tile([P, T], U8, name="scale_rows", align_bytes=64)
 
+        runs = V // P
+        frac_rows = keep.tile([P, P], F32, name="frac_rows")
+        nc.vector.memset(frac_rows[:], 0.0)
         nc.vector.memset(scale_rows[:].bitcast(I32), 0)
         nc.sync.dma_start(out=w_raw[:], in_=w1.rearrange("(p j) m -> p j m", j=PACK))
         nc.sync.dma_start(offs_sb[:], offs)
         words_hbm = x_words[0].rearrange("p n t -> p (n t)").bitcast(I32)
         for a in range(0, 2 * HEAD, HEAD):
             nc.sync.dma_start(out=words[:, a : a + HEAD], in_=words_hbm[:, a : a + HEAD])
+        nc.sync.dma_start(out=frac_rows[0:runs, :], in_=frac[0].rearrange("(c n) -> c n", n=P))
         nc.sync.dma_start(out=scale_rows[32:96:4, :].bitcast(I32), in_=x_scales[0].bitcast(I32))
         nc.sync.dma_start(out=words[:, 2 * HEAD :], in_=words_hbm[:, 2 * HEAD :])
         nc.sync.dma_start(right_sb[:], right)
@@ -57,8 +63,19 @@ def tile_picked_lerp_none_p_kernel(
                 out=x_plane[32 * q : 32 * q + 4, :].bitcast(I32),
                 in_=picked_scales[32 + 16 * q : 48 + 16 * q : 4, :].bitcast(I32),
             )
-        frac_sb = keep.tile([P, V], F32, name="frac_sb", tag="shared", align_bytes=64)
-        nc.sync.dma_start(out=frac_sb[:], in_=frac)
+        ident = keep.tile([P, P], F32, name="ident")
+        make_identity(nc, ident[:])
+        turned = psum.tile([P, P], F32, name="turned")
+        nc.tensor.transpose(turned[:], frac_rows[:], ident[:])
+        frac_cols = keep.tile([P, runs], F32, name="frac_cols")
+        nc.scalar.copy(frac_cols[:], turned[:, 0:runs])
+        spread = psum.tile([P, V], F32, name="spread")
+        for c in range(runs):
+            nc.tensor.transpose(spread[:, c * P : (c + 1) * P], frac_cols[:, c : c + 1].to_broadcast([P, P]), ident[:])
+        frac_sb = keep.tile([P, V], F32, name="frac_sb", align_bytes=64)
+        nc.scalar.copy(frac_sb[:], spread[:])
+        rest = keep.tile([P, V], F32, name="rest", align_bytes=64)
+        nc.scalar.activation(rest[:], spread[:], COPY, bias=1.0, scale=-1.0)
 
         w_bf = keep.tile([P, M, PACK], BF16, name="w_bf", align_bytes=64)
         nc.scalar.copy(w_bf[:], w_raw[:].rearrange("p j m -> p m j"))
@@ -68,12 +85,14 @@ def tile_picked_lerp_none_p_kernel(
             out=w_codes[:].bitcast(FP8X4), scales=w_plane[:], in_=w_bf[:].rearrange("p m j -> p (m j)")
         )
 
-        picked = keep.tile([P, S], U32, name="picked", align_bytes=64)
+        picked = (
+            keep.tile([P, S // 2], U32, name="picked0", align_bytes=64),
+            keep.tile([P, S // 2], U32, name="picked1", align_bytes=64),
+        )
         y = keep.tile([P, S], F32, name="y", align_bytes=64)
-        rest = keep.tile([P, V], F32, name="rest")
 
         def gather_words(a, b):
-            nc.vector.tensor_copy(picked[:, a:b], words[:].bitcast(U32).indirect(offs_sb[:, a // LANES : b // LANES]))
+            nc.vector.tensor_copy(picked[a // 512][:], words[:].bitcast(U32).indirect(offs_sb[:, a // LANES : b // LANES]))
 
         def project(a, b):
             acc = psum.tile([M, b - a], F32, name="acc%d" % a)
@@ -81,7 +100,7 @@ def tile_picked_lerp_none_p_kernel(
                 out=acc[:],
                 lhsT=w_codes[:].bitcast(FP8X4),
                 lhsT_scale=w_plane[:],
-                rhs=picked[:, a:b].bitcast(FP8X4),
+                rhs=picked[a // 512][:, a % 512 : a % 512 + b - a].bitcast(FP8X4),
                 rhs_scale=x_plane[:, a:b],
                 start=True,
                 stop=True,
@@ -89,11 +108,12 @@ def tile_picked_lerp_none_p_kernel(
             return acc
 
         gather_words(0, 512)
-        nc.scalar.copy(y[:, 0:512], project(0, 512)[:])
+        for a in (0, 256):
+            nc.scalar.copy(y[:, a : a + 256], project(a, a + 256)[:])
         gather_words(512, 1024)
-        nc.vector.tensor_scalar(rest[:], frac_sb[:], -1.0, 1.0, MULT, ADD)
-        for a in range(512, 1024, 128):
-            nc.scalar.copy(y[:, a : a + 128], project(a, a + 128)[:])
+        for a in (512, 768):
+            nc.vector.tensor_copy(y[:, a : a + 128], project(a, a + 128)[:])
+            nc.scalar.copy(y[:, a + 128 : a + 256], project(a + 128, a + 256)[:])
 
         from_right = keep.tile([P, V], F32, name="from_right")
         from_left = keep.tile([P, V], F32, name="from_left")

@@ -59,7 +59,7 @@ def tile_picked_lerp_none_p_kernel(
         picked_scales = keep.tile([P, S], U8, name="picked_scales", align_bytes=64)
         nc.vector.tensor_copy(picked_scales[:], scale_rows[:].indirect(offs_sb[:]))
         for q in range(4):
-            nc.sync.dma_start(
+            nc.scalar.dma_start(
                 out=x_plane[32 * q : 32 * q + 4, :].bitcast(I32),
                 in_=picked_scales[32 + 16 * q : 48 + 16 * q : 4, :].bitcast(I32),
             )

@@ -1,7 +1,6 @@
 from contextlib import ExitStack
 
 import concourse.mybir as mybir
-from concourse.masks import make_identity
 
 K, T, S, V, M = 512, 4096, 1024, 512, 128
 FLOPS = 2 * K * M * S
@@ -20,7 +19,7 @@ COPY = mybir.ActivationFunctionType.Copy
 P = 128
 PACK = 4
 LANES = 16
-HEAD = 448
+HEAD = 384
 
 
 def tile_picked_lerp_none_p_kernel(
@@ -36,20 +35,15 @@ def tile_picked_lerp_none_p_kernel(
         right_sb = keep.tile([P, V // LANES], U16, name="right_sb")
         w_raw = keep.tile([P, PACK, M], F32, name="w_raw")
         words = keep.tile([P, T], I32, name="words", align_bytes=64)
-        scale_rows = keep.tile([P, T], U8, name="scale_rows", align_bytes=64)
+        scale_rows = keep.tile([P, T], U8, name="scale_rows", tag="early_late", align_bytes=64)
 
-        runs = V // P
-        frac_rows = keep.tile([P, P], F32, name="frac_rows")
-        nc.vector.memset(frac_rows[:], 0.0)
         nc.vector.memset(scale_rows[:].bitcast(I32), 0)
         nc.sync.dma_start(out=w_raw[:], in_=w1.rearrange("(p j) m -> p j m", j=PACK))
         nc.sync.dma_start(offs_sb[:], offs)
         words_hbm = x_words[0].rearrange("p n t -> p (n t)").bitcast(I32)
-        for a in range(0, 2 * HEAD, HEAD):
-            nc.sync.dma_start(out=words[:, a : a + HEAD], in_=words_hbm[:, a : a + HEAD])
-        nc.sync.dma_start(out=frac_rows[0:runs, :], in_=frac[0].rearrange("(c n) -> c n", n=P))
+        nc.sync.dma_start(out=words[:, :HEAD], in_=words_hbm[:, :HEAD])
         nc.sync.dma_start(out=scale_rows[32:96:4, :].bitcast(I32), in_=x_scales[0].bitcast(I32))
-        nc.sync.dma_start(out=words[:, 2 * HEAD :], in_=words_hbm[:, 2 * HEAD :])
+        nc.sync.dma_start(out=words[:, HEAD:], in_=words_hbm[:, HEAD:])
         nc.sync.dma_start(right_sb[:], right)
         nc.sync.dma_start(left_sb[:], left)
 
@@ -59,23 +53,14 @@ def tile_picked_lerp_none_p_kernel(
         picked_scales = keep.tile([P, S], U8, name="picked_scales", align_bytes=64)
         nc.vector.tensor_copy(picked_scales[:], scale_rows[:].indirect(offs_sb[:]))
         for q in range(4):
-            nc.scalar.dma_start(
+            nc.sync.dma_start(
                 out=x_plane[32 * q : 32 * q + 4, :].bitcast(I32),
                 in_=picked_scales[32 + 16 * q : 48 + 16 * q : 4, :].bitcast(I32),
             )
-        ident = keep.tile([P, P], F32, name="ident")
-        make_identity(nc, ident[:])
-        turned = psum.tile([P, P], F32, name="turned")
-        nc.tensor.transpose(turned[:], frac_rows[:], ident[:])
-        frac_cols = keep.tile([P, runs], F32, name="frac_cols")
-        nc.scalar.copy(frac_cols[:], turned[:, 0:runs])
-        spread = psum.tile([P, V], F32, name="spread")
-        for c in range(runs):
-            nc.tensor.transpose(spread[:, c * P : (c + 1) * P], frac_cols[:, c : c + 1].to_broadcast([P, P]), ident[:])
-        frac_sb = keep.tile([P, V], F32, name="frac_sb", align_bytes=64)
-        nc.scalar.copy(frac_sb[:], spread[:])
+        frac_sb = keep.tile([P, V], F32, name="frac_sb", tag="early_late", align_bytes=64)
+        nc.sync.dma_start(out=frac_sb[:], in_=frac)
         rest = keep.tile([P, V], F32, name="rest", align_bytes=64)
-        nc.scalar.activation(rest[:], spread[:], COPY, bias=1.0, scale=-1.0)
+        nc.scalar.activation(rest[:], frac_sb[:], COPY, bias=1.0, scale=-1.0)
 
         w_bf = keep.tile([P, M, PACK], BF16, name="w_bf", align_bytes=64)
         nc.scalar.copy(w_bf[:], w_raw[:].rearrange("p j m -> p m j"))

@@ -19,7 +19,7 @@ COPY = mybir.ActivationFunctionType.Copy
 P = 128
 PACK = 4
 LANES = 16
-HEAD = 384
+HEAD = 768
 
 
 def tile_picked_lerp_none_p_kernel(
@@ -58,9 +58,9 @@ def tile_picked_lerp_none_p_kernel(
                 in_=picked_scales[32 + 16 * q : 48 + 16 * q : 4, :].bitcast(I32),
             )
         frac_sb = keep.tile([P, V], F32, name="frac_sb", tag="early_late", align_bytes=64)
-        nc.sync.dma_start(out=frac_sb[:], in_=frac)
-        rest = keep.tile([P, V], F32, name="rest", align_bytes=64)
-        nc.scalar.activation(rest[:], frac_sb[:], COPY, bias=1.0, scale=-1.0)
+        halves = ((0, V // 2), (V // 2, V))
+        for a, b in halves:
+            nc.sync.dma_start(out=frac_sb[:, a:b], in_=frac[:, a:b])
 
         w_bf = keep.tile([P, M, PACK], BF16, name="w_bf", align_bytes=64)
         nc.scalar.copy(w_bf[:], w_raw[:].rearrange("p j m -> p m j"))
@@ -72,7 +72,7 @@ def tile_picked_lerp_none_p_kernel(
 
         picked = (
             keep.tile([P, S // 2], U32, name="picked0", align_bytes=64),
-            keep.tile([P, S // 2], U32, name="picked1", align_bytes=64),
+            keep.tile([P, S // 2], U32, name="picked1", tag="picked_rest", align_bytes=64),
         )
         y = keep.tile([P, S], F32, name="y", align_bytes=64)
 
@@ -99,12 +99,13 @@ def tile_picked_lerp_none_p_kernel(
         for a in (512, 768):
             nc.vector.tensor_copy(y[:, a : a + 128], project(a, a + 128)[:])
             nc.scalar.copy(y[:, a + 128 : a + 256], project(a + 128, a + 256)[:])
+        rest = keep.tile([P, V], F32, name="rest", tag="picked_rest", align_bytes=64)
+        nc.scalar.activation(rest[:], frac_sb[:], COPY, bias=1.0, scale=-1.0)
 
         from_right = keep.tile([P, V], F32, name="from_right")
         from_left = keep.tile([P, V], F32, name="from_left")
         result = keep.tile([P, V], F32, name="result")
         nc.vector.tensor_tensor(from_right[:], y[:].indirect(right_sb[:]), frac_sb[:], MULT)
-        halves = ((0, 256), (256, 512))
         for a, b in halves:
             nc.vector.tensor_tensor(
                 from_left[:, a:b], y[:].indirect(left_sb[:, a // LANES : b // LANES]), rest[:, a:b], MULT

@@ -1,6 +1,7 @@
 from contextlib import ExitStack
 
 import concourse.mybir as mybir
+from concourse.masks import make_identity
 
 K, T, S, V, M = 512, 4096, 1024, 512, 128
 FLOPS = 2 * K * M * S
@@ -19,7 +20,7 @@ COPY = mybir.ActivationFunctionType.Copy
 P = 128
 PACK = 4
 LANES = 16
-HEAD = 768
+HEAD = 1408
 
 
 def tile_picked_lerp_none_p_kernel(
@@ -33,17 +34,26 @@ def tile_picked_lerp_none_p_kernel(
         offs_sb = keep.tile([P, S // LANES], U16, name="offs_sb")
         left_sb = keep.tile([P, V // LANES], U16, name="left_sb")
         right_sb = keep.tile([P, V // LANES], U16, name="right_sb")
-        w_raw = keep.tile([P, PACK, M], F32, name="w_raw")
+        w_raw = keep.tile([P, PACK, M], F32, name="w_raw", tag="w_picked", align_bytes=64)
         words = keep.tile([P, T], I32, name="words", align_bytes=64)
-        scale_rows = keep.tile([P, T], U8, name="scale_rows", tag="early_late", align_bytes=64)
+        scale_rows = keep.tile([P, T], U8, name="scale_rows", align_bytes=64)
 
-        nc.vector.memset(scale_rows[:].bitcast(I32), 0)
-        nc.sync.dma_start(out=w_raw[:], in_=w1.rearrange("(p j) m -> p j m", j=PACK))
-        nc.sync.dma_start(offs_sb[:], offs)
+        scale_halves = ((0, T // 2), (T // 2, T))
+        for a, b in scale_halves:
+            nc.vector.memset(scale_rows[:, a:b].bitcast(I32), 0)
+        runs = V // P
+        frac_rows = keep.tile([P, P], F32, name="frac_rows")
+        nc.vector.memset(frac_rows[:], 0.0)
+        ident = keep.tile([P, P], F32, name="ident")
+        nc.vector.memset(ident[:], 0.0)
         words_hbm = x_words[0].rearrange("p n t -> p (n t)").bitcast(I32)
         nc.sync.dma_start(out=words[:, :HEAD], in_=words_hbm[:, :HEAD])
-        nc.sync.dma_start(out=scale_rows[32:96:4, :].bitcast(I32), in_=x_scales[0].bitcast(I32))
+        nc.sync.dma_start(offs_sb[:], offs)
+        for a, b in scale_halves:
+            nc.sync.dma_start(out=scale_rows[32:96:4, a:b].bitcast(I32), in_=x_scales[0, :, a:b].bitcast(I32))
+        nc.sync.dma_start(out=frac_rows[0:runs, :], in_=frac[0].rearrange("(c n) -> c n", n=P))
         nc.sync.dma_start(out=words[:, HEAD:], in_=words_hbm[:, HEAD:])
+        nc.sync.dma_start(out=w_raw[:], in_=w1.rearrange("(p j) m -> p j m", j=PACK))
         nc.sync.dma_start(right_sb[:], right)
         nc.sync.dma_start(left_sb[:], left)
 
@@ -57,22 +67,33 @@ def tile_picked_lerp_none_p_kernel(
                 out=x_plane[32 * q : 32 * q + 4, :].bitcast(I32),
                 in_=picked_scales[32 + 16 * q : 48 + 16 * q : 4, :].bitcast(I32),
             )
-        frac_sb = keep.tile([P, V], F32, name="frac_sb", tag="early_late", align_bytes=64)
+        make_identity(nc, ident[:], nomemset=True)
+        turned = psum.tile([P, P], F32, name="turned")
+        nc.tensor.transpose(turned[:], frac_rows[:], ident[:])
+        frac_cols = keep.tile([P, runs], F32, name="frac_cols")
+        nc.scalar.copy(frac_cols[:], turned[:, 0:runs])
+        spread = psum.tile([P, V], F32, name="spread")
+        for c in range(runs):
+            nc.tensor.transpose(spread[:, c * P : (c + 1) * P], frac_cols[:, c : c + 1].to_broadcast([P, P]), ident[:])
+        frac_sb = keep.tile([P, V], F32, name="frac_sb", align_bytes=64)
+        nc.scalar.copy(frac_sb[:], spread[:])
+        rest = keep.tile([P, V], F32, name="rest", align_bytes=64)
+        nc.scalar.activation(rest[:], spread[:], COPY, bias=1.0, scale=-1.0)
         halves = ((0, V // 2), (V // 2, V))
-        for a, b in halves:
-            nc.sync.dma_start(out=frac_sb[:, a:b], in_=frac[:, a:b])
 
         w_bf = keep.tile([P, M, PACK], BF16, name="w_bf", align_bytes=64)
-        nc.scalar.copy(w_bf[:], w_raw[:].rearrange("p j m -> p m j"))
         w_codes = keep.tile([P, M], U32, name="w_codes", align_bytes=64)
         w_plane = keep.tile([P, M], U8, name="w_plane", align_bytes=64)
-        nc.vector.quantize_mx(
-            out=w_codes[:].bitcast(FP8X4), scales=w_plane[:], in_=w_bf[:].rearrange("p m j -> p (m j)")
-        )
+        w_halves = ((0, M // 2), (M // 2, M))
+        for a, b in w_halves:
+            nc.scalar.copy(
+                w_bf[:, a:b, :].rearrange("p (c i) j -> p c j i", i=4),
+                w_raw[:, :, a:b].rearrange("p j (c i) -> p c j i", i=4),
+            )
 
         picked = (
             keep.tile([P, S // 2], U32, name="picked0", align_bytes=64),
-            keep.tile([P, S // 2], U32, name="picked1", tag="picked_rest", align_bytes=64),
+            keep.tile([P, S // 2], U32, name="picked1", tag="w_picked", align_bytes=64),
         )
         y = keep.tile([P, S], F32, name="y", align_bytes=64)
 
@@ -93,14 +114,18 @@ def tile_picked_lerp_none_p_kernel(
             return acc
 
         gather_words(0, 512)
+        for a, b in w_halves:
+            nc.vector.quantize_mx(
+                out=w_codes[:, a:b].bitcast(FP8X4),
+                scales=w_plane[:, a:b],
+                in_=w_bf[:, a:b, :].rearrange("p m j -> p (m j)"),
+            )
         for a in (0, 256):
             nc.scalar.copy(y[:, a : a + 256], project(a, a + 256)[:])
         gather_words(512, 1024)
         for a in (512, 768):
             nc.vector.tensor_copy(y[:, a : a + 128], project(a, a + 128)[:])
             nc.scalar.copy(y[:, a + 128 : a + 256], project(a + 128, a + 256)[:])
-        rest = keep.tile([P, V], F32, name="rest", tag="picked_rest", align_bytes=64)
-        nc.scalar.activation(rest[:], frac_sb[:], COPY, bias=1.0, scale=-1.0)
 
         from_right = keep.tile([P, V], F32, name="from_right")
         from_left = keep.tile([P, V], F32, name="from_left")

@@ -20,7 +20,7 @@ COPY = mybir.ActivationFunctionType.Copy
 P = 128
 PACK = 4
 LANES = 16
-HEAD = 1408
+HEAD = 896
 
 
 def tile_picked_lerp_none_p_kernel(

@@ -21,6 +21,7 @@ P = 128
 PACK = 4
 LANES = 16
 HEAD = 896
+SCALAR_SHARE = 72
 
 
 def tile_picked_lerp_none_p_kernel(
@@ -84,12 +85,13 @@ def tile_picked_lerp_none_p_kernel(
         w_bf = keep.tile([P, M, PACK], BF16, name="w_bf", align_bytes=64)
         w_codes = keep.tile([P, M], U32, name="w_codes", align_bytes=64)
         w_plane = keep.tile([P, M], U8, name="w_plane", align_bytes=64)
-        w_halves = ((0, M // 2), (M // 2, M))
-        for a, b in w_halves:
-            nc.scalar.copy(
-                w_bf[:, a:b, :].rearrange("p (c i) j -> p c j i", i=4),
-                w_raw[:, :, a:b].rearrange("p j (c i) -> p c j i", i=4),
-            )
+        nc.scalar.copy(
+            w_bf[:, :SCALAR_SHARE, :].rearrange("p (c i) j -> p c j i", i=4),
+            w_raw[:, :, :SCALAR_SHARE].rearrange("p j (c i) -> p c j i", i=4),
+        )
+        nc.gpsimd.tensor_scalar(
+            w_bf[:, SCALAR_SHARE:, :], w_raw[:, :, SCALAR_SHARE:].rearrange("p j m -> p m j"), 1.0, 0.0, MULT, ADD
+        )
 
         picked = (
             keep.tile([P, S // 2], U32, name="picked0", align_bytes=64),
@@ -114,12 +116,9 @@ def tile_picked_lerp_none_p_kernel(
             return acc
 
         gather_words(0, 512)
-        for a, b in w_halves:
-            nc.vector.quantize_mx(
-                out=w_codes[:, a:b].bitcast(FP8X4),
-                scales=w_plane[:, a:b],
-                in_=w_bf[:, a:b, :].rearrange("p m j -> p (m j)"),
-            )
+        nc.vector.quantize_mx(
+            out=w_codes[:].bitcast(FP8X4), scales=w_plane[:], in_=w_bf[:].rearrange("p m j -> p (m j)")
+        )
         for a in (0, 256):
             nc.scalar.copy(y[:, a : a + 256], project(a, a + 256)[:])
         gather_words(512, 1024)

@@ -20,8 +20,8 @@ COPY = mybir.ActivationFunctionType.Copy
 P = 128
 PACK = 4
 LANES = 16
-HEAD = 896
-SCALAR_SHARE = 72
+HEAD = 768
+SCALAR_SHARE = 40
 
 
 def tile_picked_lerp_none_p_kernel(
@@ -35,7 +35,11 @@ def tile_picked_lerp_none_p_kernel(
         offs_sb = keep.tile([P, S // LANES], U16, name="offs_sb")
         left_sb = keep.tile([P, V // LANES], U16, name="left_sb")
         right_sb = keep.tile([P, V // LANES], U16, name="right_sb")
-        w_raw = keep.tile([P, PACK, M], F32, name="w_raw", tag="w_picked", align_bytes=64)
+        w_halves = (
+            keep.tile([P, PACK, M // 2], F32, name="w_early", align_bytes=64),
+            keep.tile([P, PACK, M // 2], F32, name="w_late", tag="w_picked", align_bytes=64),
+        )
+        w_hbm = w1.rearrange("(p j) m -> p j m", j=PACK)
         words = keep.tile([P, T], I32, name="words", align_bytes=64)
         scale_rows = keep.tile([P, T], U8, name="scale_rows", align_bytes=64)
 
@@ -48,15 +52,46 @@ def tile_picked_lerp_none_p_kernel(
         ident = keep.tile([P, P], F32, name="ident")
         nc.vector.memset(ident[:], 0.0)
         words_hbm = x_words[0].rearrange("p n t -> p (n t)").bitcast(I32)
+        nc.sync.dma_start(out=w_halves[0][:], in_=w_hbm[:, :, : M // 2])
         nc.sync.dma_start(out=words[:, :HEAD], in_=words_hbm[:, :HEAD])
         nc.sync.dma_start(offs_sb[:], offs)
         for a, b in scale_halves:
             nc.sync.dma_start(out=scale_rows[32:96:4, a:b].bitcast(I32), in_=x_scales[0, :, a:b].bitcast(I32))
         nc.sync.dma_start(out=frac_rows[0:runs, :], in_=frac[0].rearrange("(c n) -> c n", n=P))
         nc.sync.dma_start(out=words[:, HEAD:], in_=words_hbm[:, HEAD:])
-        nc.sync.dma_start(out=w_raw[:], in_=w1.rearrange("(p j) m -> p j m", j=PACK))
+        nc.sync.dma_start(out=w_halves[1][:], in_=w_hbm[:, :, M // 2 :])
         nc.sync.dma_start(right_sb[:], right)
         nc.sync.dma_start(left_sb[:], left)
+
+        w_codes = keep.tile([P, M], U32, name="w_codes", align_bytes=64)
+        w_plane = keep.tile([P, M], U8, name="w_plane", align_bytes=64)
+        w_bf = [keep.tile([P, M // 2, PACK], BF16, name="w_bf%d" % h, align_bytes=64) for h in range(2)]
+
+        def round_and_weave(h, scalar_share):
+            nc.scalar.copy(
+                w_bf[h][:, :scalar_share, :].rearrange("p (c i) j -> p c j i", i=4),
+                w_halves[h][:, :, :scalar_share].rearrange("p j (c i) -> p c j i", i=4),
+            )
+            if scalar_share < M // 2:
+                nc.gpsimd.tensor_scalar(
+                    w_bf[h][:, scalar_share:, :],
+                    w_halves[h][:, :, scalar_share:].rearrange("p j m -> p m j"),
+                    1.0,
+                    0.0,
+                    MULT,
+                    ADD,
+                )
+
+        def quantise(h):
+            cols = slice(h * M // 2, (h + 1) * M // 2)
+            nc.vector.quantize_mx(
+                out=w_codes[:, cols].bitcast(FP8X4),
+                scales=w_plane[:, cols],
+                in_=w_bf[h][:].rearrange("p m j -> p (m j)"),
+            )
+
+        round_and_weave(0, M // 2)
+        quantise(0)
 
         x_plane = keep.tile([P, S], U8, name="x_plane", align_bytes=64)
         nc.vector.memset(x_plane[:].bitcast(I32), 0)
@@ -82,16 +117,8 @@ def tile_picked_lerp_none_p_kernel(
         nc.scalar.activation(rest[:], spread[:], COPY, bias=1.0, scale=-1.0)
         halves = ((0, V // 2), (V // 2, V))
 
-        w_bf = keep.tile([P, M, PACK], BF16, name="w_bf", align_bytes=64)
-        w_codes = keep.tile([P, M], U32, name="w_codes", align_bytes=64)
-        w_plane = keep.tile([P, M], U8, name="w_plane", align_bytes=64)
-        nc.scalar.copy(
-            w_bf[:, :SCALAR_SHARE, :].rearrange("p (c i) j -> p c j i", i=4),
-            w_raw[:, :, :SCALAR_SHARE].rearrange("p j (c i) -> p c j i", i=4),
-        )
-        nc.gpsimd.tensor_scalar(
-            w_bf[:, SCALAR_SHARE:, :], w_raw[:, :, SCALAR_SHARE:].rearrange("p j m -> p m j"), 1.0, 0.0, MULT, ADD
-        )
+
+        round_and_weave(1, SCALAR_SHARE)
 
         picked = (
             keep.tile([P, S // 2], U32, name="picked0", align_bytes=64),
@@ -116,9 +143,7 @@ def tile_picked_lerp_none_p_kernel(
             return acc
 
         gather_words(0, 512)
-        nc.vector.quantize_mx(
-            out=w_codes[:].bitcast(FP8X4), scales=w_plane[:], in_=w_bf[:].rearrange("p m j -> p (m j)")
-        )
+        quantise(1)
         for a in (0, 256):
             nc.scalar.copy(y[:, a : a + 256], project(a, a + 256)[:])
         gather_words(512, 1024)

@@ -147,9 +147,9 @@ def tile_picked_lerp_none_p_kernel(
         for a in (0, 256):
             nc.scalar.copy(y[:, a : a + 256], project(a, a + 256)[:])
         gather_words(512, 1024)
-        for a in (512, 768):
-            nc.vector.tensor_copy(y[:, a : a + 128], project(a, a + 128)[:])
-            nc.scalar.copy(y[:, a + 128 : a + 256], project(a + 128, a + 256)[:])
+        nc.vector.tensor_copy(y[:, 512:768], project(512, 768)[:])
+        for a in (768, 896):
+            nc.scalar.copy(y[:, a : a + 128], project(a, a + 128)[:])
 
         from_right = keep.tile([P, V], F32, name="from_right")
         from_left = keep.tile([P, V], F32, name="from_left")

@@ -127,7 +127,10 @@ def tile_picked_lerp_none_p_kernel(
         y = keep.tile([P, S], F32, name="y", align_bytes=64)
 
         def gather_words(a, b):
-            nc.vector.tensor_copy(picked[a // 512][:], words[:].bitcast(U32).indirect(offs_sb[:, a // LANES : b // LANES]))
+            nc.vector.tensor_copy(
+                picked[a // 512][:, a % 512 : a % 512 + b - a],
+                words[:].bitcast(U32).indirect(offs_sb[:, a // LANES : b // LANES]),
+            )
 
         def project(a, b):
             acc = psum.tile([M, b - a], F32, name="acc%d" % a)
@@ -146,19 +149,21 @@ def tile_picked_lerp_none_p_kernel(
         quantise(1)
         for a in (0, 256):
             nc.scalar.copy(y[:, a : a + 256], project(a, a + 256)[:])
-        gather_words(512, 1024)
-        nc.vector.tensor_copy(y[:, 512:768], project(512, 768)[:])
-        for a in (768, 896):
-            nc.scalar.copy(y[:, a : a + 128], project(a, a + 128)[:])
+        gather_words(512, 768)
+        nc.scalar.copy(y[:, 512:768], project(512, 768)[:])
+        gather_words(768, 1024)
+        nc.vector.tensor_copy(y[:, 768:896], project(768, 896)[:])
+        nc.scalar.copy(y[:, 896:1024], project(896, 1024)[:])
 
         from_right = keep.tile([P, V], F32, name="from_right")
+        at_left = keep.tile([P, V], F32, name="at_left")
         from_left = keep.tile([P, V], F32, name="from_left")
         result = keep.tile([P, V], F32, name="result")
+        for a, b in halves:
+            nc.scalar.activation(at_left[:, a:b], y[:].indirect(left_sb[:, a // LANES : b // LANES]), COPY)
         nc.vector.tensor_tensor(from_right[:], y[:].indirect(right_sb[:]), frac_sb[:], MULT)
         for a, b in halves:
-            nc.vector.tensor_tensor(
-                from_left[:, a:b], y[:].indirect(left_sb[:, a // LANES : b // LANES]), rest[:, a:b], MULT
-            )
+            nc.vector.tensor_tensor(from_left[:, a:b], at_left[:, a:b], rest[:, a:b], MULT)
         for (a, b), queue in zip(halves, (nc.sync, nc.scalar)):
             nc.vector.tensor_tensor(result[:, a:b], from_left[:, a:b], from_right[:, a:b], ADD)
             queue.dma_start(out=out[:, a:b], in_=result[:, a:b])

@@ -107,16 +107,19 @@ def tile_picked_lerp_none_p_kernel(
         turned = psum.tile([P, P], F32, name="turned")
         nc.tensor.transpose(turned[:], frac_rows[:], ident[:])
         frac_cols = keep.tile([P, runs], F32, name="frac_cols")
+        rest_cols = keep.tile([P, runs], F32, name="rest_cols")
         nc.scalar.copy(frac_cols[:], turned[:, 0:runs])
+        nc.scalar.activation(rest_cols[:], turned[:, 0:runs], COPY, bias=1.0, scale=-1.0)
         spread = psum.tile([P, V], F32, name="spread")
-        for c in range(runs):
-            nc.tensor.transpose(spread[:, c * P : (c + 1) * P], frac_cols[:, c : c + 1].to_broadcast([P, P]), ident[:])
+        rest_bank = psum.tile([P, V], F32, name="rest_bank")
+        for bank, cols in ((spread, frac_cols), (rest_bank, rest_cols)):
+            for c in range(runs):
+                nc.tensor.transpose(bank[:, c * P : (c + 1) * P], cols[:, c : c + 1].to_broadcast([P, P]), ident[:])
         frac_sb = keep.tile([P, V], F32, name="frac_sb", align_bytes=64)
         nc.scalar.copy(frac_sb[:], spread[:])
-        rest = keep.tile([P, V], F32, name="rest", align_bytes=64)
-        nc.scalar.activation(rest[:], spread[:], COPY, bias=1.0, scale=-1.0)
-        halves = ((0, V // 2), (V // 2, V))
-
+        first, middle, last = (0, 256), (256, 384), (384, V)
+        rest_middle = keep.tile([P, middle[1] - middle[0]], F32, name="rest_middle", align_bytes=64)
+        nc.scalar.copy(rest_middle[:], rest_bank[:, middle[0] : middle[1]])
 
         round_and_weave(1, SCALAR_SHARE)
 
@@ -159,11 +162,13 @@ def tile_picked_lerp_none_p_kernel(
         at_left = keep.tile([P, V], F32, name="at_left")
         from_left = keep.tile([P, V], F32, name="from_left")
         result = keep.tile([P, V], F32, name="result")
-        for a, b in halves:
+        for a, b in ((0, last[0]), last):
             nc.scalar.activation(at_left[:, a:b], y[:].indirect(left_sb[:, a // LANES : b // LANES]), COPY)
         nc.vector.tensor_tensor(from_right[:], y[:].indirect(right_sb[:]), frac_sb[:], MULT)
-        for a, b in halves:
-            nc.vector.tensor_tensor(from_left[:, a:b], at_left[:, a:b], rest[:, a:b], MULT)
-        for (a, b), queue in zip(halves, (nc.sync, nc.scalar)):
+        nc.gpsimd.tensor_tensor(from_left[:, middle[0] : middle[1]], at_left[:, middle[0] : middle[1]], rest_middle[:], MULT)
+        for a, b in ((0, 128), (128, 256), last):
+            nc.vector.tensor_tensor(from_left[:, a:b], at_left[:, a:b], rest_bank[:, a:b], MULT)
+        for a, b in ((0, 128), (128, 256), (256, V)):
             nc.vector.tensor_tensor(result[:, a:b], from_left[:, a:b], from_right[:, a:b], ADD)
+        for (a, b), queue in zip(((0, V // 2), (V // 2, V)), (nc.sync, nc.scalar)):
             queue.dma_start(out=out[:, a:b], in_=result[:, a:b])

@@ -20,7 +20,7 @@ COPY = mybir.ActivationFunctionType.Copy
 P = 128
 PACK = 4
 LANES = 16
-HEAD = 768
+HEAD = 896
 SCALAR_SHARE = 40
 
 
@@ -48,16 +48,16 @@ def tile_picked_lerp_none_p_kernel(
             nc.vector.memset(scale_rows[:, a:b].bitcast(I32), 0)
         runs = V // P
         frac_rows = keep.tile([P, P], F32, name="frac_rows")
-        nc.vector.memset(frac_rows[:], 0.0)
+        nc.vector.memset(frac_rows[: P - runs, :], 0.0)
         ident = keep.tile([P, P], F32, name="ident")
         nc.vector.memset(ident[:], 0.0)
         words_hbm = x_words[0].rearrange("p n t -> p (n t)").bitcast(I32)
         nc.sync.dma_start(out=w_halves[0][:], in_=w_hbm[:, :, : M // 2])
         nc.sync.dma_start(out=words[:, :HEAD], in_=words_hbm[:, :HEAD])
         nc.sync.dma_start(offs_sb[:], offs)
+        nc.sync.dma_start(out=frac_rows[P - runs :, :], in_=frac[0].rearrange("(c n) -> c n", n=P))
         for a, b in scale_halves:
             nc.sync.dma_start(out=scale_rows[32:96:4, a:b].bitcast(I32), in_=x_scales[0, :, a:b].bitcast(I32))
-        nc.sync.dma_start(out=frac_rows[0:runs, :], in_=frac[0].rearrange("(c n) -> c n", n=P))
         nc.sync.dma_start(out=words[:, HEAD:], in_=words_hbm[:, HEAD:])
         nc.sync.dma_start(out=w_halves[1][:], in_=w_hbm[:, :, M // 2 :])
         nc.sync.dma_start(right_sb[:], right)
@@ -108,8 +108,8 @@ def tile_picked_lerp_none_p_kernel(
         nc.tensor.transpose(turned[:], frac_rows[:], ident[:])
         frac_cols = keep.tile([P, runs], F32, name="frac_cols")
         rest_cols = keep.tile([P, runs], F32, name="rest_cols")
-        nc.scalar.copy(frac_cols[:], turned[:, 0:runs])
-        nc.scalar.activation(rest_cols[:], turned[:, 0:runs], COPY, bias=1.0, scale=-1.0)
+        nc.scalar.copy(frac_cols[:], turned[:, P - runs :])
+        nc.scalar.activation(rest_cols[:], turned[:, P - runs :], COPY, bias=1.0, scale=-1.0)
         spread = psum.tile([P, V], F32, name="spread")
         rest_bank = psum.tile([P, V], F32, name="rest_bank")
         for bank, cols in ((spread, frac_cols), (rest_bank, rest_cols)):

@@ -170,5 +170,5 @@ def tile_picked_lerp_none_p_kernel(
             nc.vector.tensor_tensor(from_left[:, a:b], at_left[:, a:b], rest_bank[:, a:b], MULT)
         for a, b in ((0, 128), (128, 256), (256, V)):
             nc.vector.tensor_tensor(result[:, a:b], from_left[:, a:b], from_right[:, a:b], ADD)
-        for (a, b), queue in zip(((0, V // 2), (V // 2, V)), (nc.sync, nc.scalar)):
-            queue.dma_start(out=out[:, a:b], in_=result[:, a:b])
+        for a, b in ((0, V // 2), (V // 2, V)):
+            nc.scalar.dma_start(out=out[:, a:b], in_=result[:, a:b])

@@ -20,7 +20,7 @@ COPY = mybir.ActivationFunctionType.Copy
 P = 128
 PACK = 4
 LANES = 16
-HEAD = 896
+HEAD = 576
 SCALAR_SHARE = 40
 
 
@@ -56,8 +56,8 @@ def tile_picked_lerp_none_p_kernel(
         nc.sync.dma_start(out=words[:, :HEAD], in_=words_hbm[:, :HEAD])
         nc.sync.dma_start(offs_sb[:], offs)
         nc.sync.dma_start(out=frac_rows[P - runs :, :], in_=frac[0].rearrange("(c n) -> c n", n=P))
-        for a, b in scale_halves:
-            nc.sync.dma_start(out=scale_rows[32:96:4, a:b].bitcast(I32), in_=x_scales[0, :, a:b].bitcast(I32))
+        for (a, b), queue in zip(scale_halves, (nc.sync, nc.scalar)):
+            queue.dma_start(out=scale_rows[32:96:4, a:b].bitcast(I32), in_=x_scales[0, :, a:b].bitcast(I32))
         nc.sync.dma_start(out=words[:, HEAD:], in_=words_hbm[:, HEAD:])
         nc.sync.dma_start(out=w_halves[1][:], in_=w_hbm[:, :, M // 2 :])
         nc.sync.dma_start(right_sb[:], right)
@@ -72,15 +72,14 @@ def tile_picked_lerp_none_p_kernel(
                 w_bf[h][:, :scalar_share, :].rearrange("p (c i) j -> p c j i", i=4),
                 w_halves[h][:, :, :scalar_share].rearrange("p j (c i) -> p c j i", i=4),
             )
-            if scalar_share < M // 2:
-                nc.gpsimd.tensor_scalar(
-                    w_bf[h][:, scalar_share:, :],
-                    w_halves[h][:, :, scalar_share:].rearrange("p j m -> p m j"),
-                    1.0,
-                    0.0,
-                    MULT,
-                    ADD,
-                )
+            nc.gpsimd.tensor_scalar(
+                w_bf[h][:, scalar_share:, :],
+                w_halves[h][:, :, scalar_share:].rearrange("p j m -> p m j"),
+                1.0,
+                0.0,
+                MULT,
+                ADD,
+            )
 
         def quantise(h):
             cols = slice(h * M // 2, (h + 1) * M // 2)
@@ -90,7 +89,7 @@ def tile_picked_lerp_none_p_kernel(
                 in_=w_bf[h][:].rearrange("p m j -> p (m j)"),
             )
 
-        round_and_weave(0, M // 2)
+        nc.vector.tensor_copy(w_bf[0][:], w_halves[0][:].rearrange("p j m -> p m j"))
         quantise(0)
 
         x_plane = keep.tile([P, S], U8, name="x_plane", align_bytes=64)

@@ -20,7 +20,7 @@ COPY = mybir.ActivationFunctionType.Copy
 P = 128
 PACK = 4
 LANES = 16
-HEAD = 576
+HEAD = 640
 SCALAR_SHARE = 40
 
 
@@ -43,21 +43,18 @@ def tile_picked_lerp_none_p_kernel(
         words = keep.tile([P, T], I32, name="words", align_bytes=64)
         scale_rows = keep.tile([P, T], U8, name="scale_rows", align_bytes=64)
 
-        scale_halves = ((0, T // 2), (T // 2, T))
-        for a, b in scale_halves:
-            nc.vector.memset(scale_rows[:, a:b].bitcast(I32), 0)
+        nc.vector.memset(scale_rows[:].bitcast(I32), 0)
         runs = V // P
         frac_rows = keep.tile([P, P], F32, name="frac_rows")
-        nc.vector.memset(frac_rows[: P - runs, :], 0.0)
+        nc.vector.memset(frac_rows[:], 0.0)
         ident = keep.tile([P, P], F32, name="ident")
         nc.vector.memset(ident[:], 0.0)
         words_hbm = x_words[0].rearrange("p n t -> p (n t)").bitcast(I32)
         nc.sync.dma_start(out=w_halves[0][:], in_=w_hbm[:, :, : M // 2])
         nc.sync.dma_start(out=words[:, :HEAD], in_=words_hbm[:, :HEAD])
         nc.sync.dma_start(offs_sb[:], offs)
-        nc.sync.dma_start(out=frac_rows[P - runs :, :], in_=frac[0].rearrange("(c n) -> c n", n=P))
-        for (a, b), queue in zip(scale_halves, (nc.sync, nc.scalar)):
-            queue.dma_start(out=scale_rows[32:96:4, a:b].bitcast(I32), in_=x_scales[0, :, a:b].bitcast(I32))
+        nc.scalar.dma_start(out=scale_rows[32:96:4, :].bitcast(I32), in_=x_scales[0].bitcast(I32))
+        nc.sync.dma_start(out=frac_rows[:runs, :], in_=frac[0].rearrange("(c n) -> c n", n=P))
         nc.sync.dma_start(out=words[:, HEAD:], in_=words_hbm[:, HEAD:])
         nc.sync.dma_start(out=w_halves[1][:], in_=w_hbm[:, :, M // 2 :])
         nc.sync.dma_start(right_sb[:], right)
@@ -106,19 +103,15 @@ def tile_picked_lerp_none_p_kernel(
         turned = psum.tile([P, P], F32, name="turned")
         nc.tensor.transpose(turned[:], frac_rows[:], ident[:])
         frac_cols = keep.tile([P, runs], F32, name="frac_cols")
-        rest_cols = keep.tile([P, runs], F32, name="rest_cols")
-        nc.scalar.copy(frac_cols[:], turned[:, P - runs :])
-        nc.scalar.activation(rest_cols[:], turned[:, P - runs :], COPY, bias=1.0, scale=-1.0)
-        spread = psum.tile([P, V], F32, name="spread")
-        rest_bank = psum.tile([P, V], F32, name="rest_bank")
-        for bank, cols in ((spread, frac_cols), (rest_bank, rest_cols)):
-            for c in range(runs):
-                nc.tensor.transpose(bank[:, c * P : (c + 1) * P], cols[:, c : c + 1].to_broadcast([P, P]), ident[:])
-        frac_sb = keep.tile([P, V], F32, name="frac_sb", align_bytes=64)
-        nc.scalar.copy(frac_sb[:], spread[:])
-        first, middle, last = (0, 256), (256, 384), (384, V)
-        rest_middle = keep.tile([P, middle[1] - middle[0]], F32, name="rest_middle", align_bytes=64)
-        nc.scalar.copy(rest_middle[:], rest_bank[:, middle[0] : middle[1]])
+        nc.scalar.copy(frac_cols[:], turned[:, :runs])
+        frac_bank = psum.tile([P, V], F32, name="frac_bank")
+        for c in range(runs):
+            nc.tensor.transpose(frac_bank[:, c * P : (c + 1) * P], frac_cols[:, c : c + 1].to_broadcast([P, P]), ident[:])
+        rest_sb = keep.tile([P, V], F32, name="rest_sb", align_bytes=64)
+        nc.scalar.activation(rest_sb[:], frac_bank[:], COPY, bias=1.0, scale=-1.0)
+        middle, last = (256, 384), (384, V)
+        frac_middle = keep.tile([P, middle[1] - middle[0]], F32, name="frac_middle", align_bytes=64)
+        nc.scalar.copy(frac_middle[:], frac_bank[:, middle[0] : middle[1]])
 
         round_and_weave(1, SCALAR_SHARE)
 
@@ -157,16 +150,16 @@ def tile_picked_lerp_none_p_kernel(
         nc.vector.tensor_copy(y[:, 768:896], project(768, 896)[:])
         nc.scalar.copy(y[:, 896:1024], project(896, 1024)[:])
 
-        from_right = keep.tile([P, V], F32, name="from_right")
-        at_left = keep.tile([P, V], F32, name="at_left")
         from_left = keep.tile([P, V], F32, name="from_left")
+        at_right = keep.tile([P, V], F32, name="at_right")
+        from_right = keep.tile([P, V], F32, name="from_right")
         result = keep.tile([P, V], F32, name="result")
         for a, b in ((0, last[0]), last):
-            nc.scalar.activation(at_left[:, a:b], y[:].indirect(left_sb[:, a // LANES : b // LANES]), COPY)
-        nc.vector.tensor_tensor(from_right[:], y[:].indirect(right_sb[:]), frac_sb[:], MULT)
-        nc.gpsimd.tensor_tensor(from_left[:, middle[0] : middle[1]], at_left[:, middle[0] : middle[1]], rest_middle[:], MULT)
+            nc.scalar.activation(at_right[:, a:b], y[:].indirect(right_sb[:, a // LANES : b // LANES]), COPY)
+        nc.vector.tensor_tensor(from_left[:], y[:].indirect(left_sb[:]), rest_sb[:], MULT)
+        nc.gpsimd.tensor_tensor(from_right[:, middle[0] : middle[1]], at_right[:, middle[0] : middle[1]], frac_middle[:], MULT)
         for a, b in ((0, 128), (128, 256), last):
-            nc.vector.tensor_tensor(from_left[:, a:b], at_left[:, a:b], rest_bank[:, a:b], MULT)
+            nc.vector.tensor_tensor(from_right[:, a:b], at_right[:, a:b], frac_bank[:, a:b], MULT)
         for a, b in ((0, 128), (128, 256), (256, V)):
             nc.vector.tensor_tensor(result[:, a:b], from_left[:, a:b], from_right[:, a:b], ADD)
         for a, b in ((0, V // 2), (V // 2, V)):

@@ -20,7 +20,7 @@ COPY = mybir.ActivationFunctionType.Copy
 P = 128
 PACK = 4
 LANES = 16
-HEAD = 640
+HEAD = 832
 SCALAR_SHARE = 40
 
 
@@ -30,6 +30,7 @@ def tile_picked_lerp_none_p_kernel(
     nc = tc.nc
     with ExitStack() as ctx:
         keep = ctx.enter_context(tc.tile_pool(name="keep", bufs=1))
+        reuse = ctx.enter_context(tc.tile_pool(name="reuse", bufs=1))
         psum = ctx.enter_context(tc.psum_pool(name="psum", bufs=1))
 
         offs_sb = keep.tile([P, S // LANES], U16, name="offs_sb")
@@ -37,87 +38,81 @@ def tile_picked_lerp_none_p_kernel(
         right_sb = keep.tile([P, V // LANES], U16, name="right_sb")
         w_halves = (
             keep.tile([P, PACK, M // 2], F32, name="w_early", align_bytes=64),
-            keep.tile([P, PACK, M // 2], F32, name="w_late", tag="w_picked", align_bytes=64),
+            reuse.tile([P, PACK, M // 2], F32, name="w_late", offset=1536, align_bytes=64),
         )
         w_hbm = w1.rearrange("(p j) m -> p j m", j=PACK)
         words = keep.tile([P, T], I32, name="words", align_bytes=64)
         scale_rows = keep.tile([P, T], U8, name="scale_rows", align_bytes=64)
 
-        nc.vector.memset(scale_rows[:].bitcast(I32), 0)
+        scale_halves = ((0, T // 2), (T // 2, T))
+        for a, b in scale_halves:
+            nc.vector.memset(scale_rows[:, a:b].bitcast(I32), 0)
         runs = V // P
-        frac_rows = keep.tile([P, P], F32, name="frac_rows")
-        nc.vector.memset(frac_rows[:], 0.0)
+        frac_rows = keep.tile([P, P], F32, name="frac_rows", tag="rows_plane", align_bytes=64)
+        nc.vector.memset(frac_rows[: P - runs, :], 0.0)
         ident = keep.tile([P, P], F32, name="ident")
         nc.vector.memset(ident[:], 0.0)
         words_hbm = x_words[0].rearrange("p n t -> p (n t)").bitcast(I32)
-        nc.sync.dma_start(out=w_halves[0][:], in_=w_hbm[:, :, : M // 2])
         nc.sync.dma_start(out=words[:, :HEAD], in_=words_hbm[:, :HEAD])
         nc.sync.dma_start(offs_sb[:], offs)
-        nc.scalar.dma_start(out=scale_rows[32:96:4, :].bitcast(I32), in_=x_scales[0].bitcast(I32))
-        nc.sync.dma_start(out=frac_rows[:runs, :], in_=frac[0].rearrange("(c n) -> c n", n=P))
+        nc.sync.dma_start(out=frac_rows[P - runs :, :], in_=frac[0].rearrange("(c n) -> c n", n=P))
+        nc.sync.dma_start(left_sb[:], left)
+        for a, b in scale_halves:
+            nc.sync.dma_start(out=scale_rows[32:96:4, a:b].bitcast(I32), in_=x_scales[0, :, a:b].bitcast(I32))
         nc.sync.dma_start(out=words[:, HEAD:], in_=words_hbm[:, HEAD:])
+        nc.sync.dma_start(out=w_halves[0][:], in_=w_hbm[:, :, : M // 2])
         nc.sync.dma_start(out=w_halves[1][:], in_=w_hbm[:, :, M // 2 :])
         nc.sync.dma_start(right_sb[:], right)
-        nc.sync.dma_start(left_sb[:], left)
 
         w_codes = keep.tile([P, M], U32, name="w_codes", align_bytes=64)
         w_plane = keep.tile([P, M], U8, name="w_plane", align_bytes=64)
-        w_bf = [keep.tile([P, M // 2, PACK], BF16, name="w_bf%d" % h, align_bytes=64) for h in range(2)]
+        w_bf = keep.tile([P, M, PACK], BF16, name="w_bf", align_bytes=64)
 
-        def round_and_weave(h, scalar_share):
+        def weave_on_scalar(h, count):
             nc.scalar.copy(
-                w_bf[h][:, :scalar_share, :].rearrange("p (c i) j -> p c j i", i=4),
-                w_halves[h][:, :, :scalar_share].rearrange("p j (c i) -> p c j i", i=4),
+                w_bf[:, h * M // 2 : h * M // 2 + count, :].rearrange("p (c i) j -> p c j i", i=4),
+                w_halves[h][:, :, :count].rearrange("p j (c i) -> p c j i", i=4),
             )
-            nc.gpsimd.tensor_scalar(
-                w_bf[h][:, scalar_share:, :],
-                w_halves[h][:, :, scalar_share:].rearrange("p j m -> p m j"),
-                1.0,
-                0.0,
-                MULT,
-                ADD,
-            )
-
-        def quantise(h):
-            cols = slice(h * M // 2, (h + 1) * M // 2)
-            nc.vector.quantize_mx(
-                out=w_codes[:, cols].bitcast(FP8X4),
-                scales=w_plane[:, cols],
-                in_=w_bf[h][:].rearrange("p m j -> p (m j)"),
-            )
-
-        nc.vector.tensor_copy(w_bf[0][:], w_halves[0][:].rearrange("p j m -> p m j"))
-        quantise(0)
-
-        x_plane = keep.tile([P, S], U8, name="x_plane", align_bytes=64)
-        nc.vector.memset(x_plane[:].bitcast(I32), 0)
 
         picked_scales = keep.tile([P, S], U8, name="picked_scales", align_bytes=64)
         nc.vector.tensor_copy(picked_scales[:], scale_rows[:].indirect(offs_sb[:]))
-        for q in range(4):
-            nc.sync.dma_start(
-                out=x_plane[32 * q : 32 * q + 4, :].bitcast(I32),
-                in_=picked_scales[32 + 16 * q : 48 + 16 * q : 4, :].bitcast(I32),
-            )
         make_identity(nc, ident[:], nomemset=True)
         turned = psum.tile([P, P], F32, name="turned")
         nc.tensor.transpose(turned[:], frac_rows[:], ident[:])
         frac_cols = keep.tile([P, runs], F32, name="frac_cols")
-        nc.scalar.copy(frac_cols[:], turned[:, :runs])
+        nc.scalar.copy(frac_cols[:], turned[:, P - runs :])
         frac_bank = psum.tile([P, V], F32, name="frac_bank")
         for c in range(runs):
             nc.tensor.transpose(frac_bank[:, c * P : (c + 1) * P], frac_cols[:, c : c + 1].to_broadcast([P, P]), ident[:])
-        rest_sb = keep.tile([P, V], F32, name="rest_sb", align_bytes=64)
-        nc.scalar.activation(rest_sb[:], frac_bank[:], COPY, bias=1.0, scale=-1.0)
         middle, last = (256, 384), (384, V)
         frac_middle = keep.tile([P, middle[1] - middle[0]], F32, name="frac_middle", align_bytes=64)
         nc.scalar.copy(frac_middle[:], frac_bank[:, middle[0] : middle[1]])
 
-        round_and_weave(1, SCALAR_SHARE)
+        x_plane = keep.tile([P, S], U8, name="x_plane", tag="rows_plane", align_bytes=64)
+        nc.gpsimd.memset(x_plane[:].bitcast(I32), 0)
+        for q, queue in enumerate((nc.sync, nc.sync, nc.sync, nc.scalar)):
+            queue.dma_start(
+                out=x_plane[32 * q : 32 * q + 4, :].bitcast(I32),
+                in_=picked_scales[32 + 16 * q : 48 + 16 * q : 4, :].bitcast(I32),
+            )
+
+        weave_on_scalar(0, M // 2)
+        weave_on_scalar(1, SCALAR_SHARE)
+        nc.gpsimd.tensor_scalar(
+            w_bf[:, M // 2 + SCALAR_SHARE :, :],
+            w_halves[1][:, :, SCALAR_SHARE:].rearrange("p j m -> p m j"),
+            1.0,
+            0.0,
+            MULT,
+            ADD,
+        )
+
+        rest_sb = reuse.tile([P, V], F32, name="rest_sb", offset=0, align_bytes=64)
+        nc.scalar.activation(rest_sb[:], frac_bank[:], COPY, bias=1.0, scale=-1.0)
 
         picked = (
             keep.tile([P, S // 2], U32, name="picked0", align_bytes=64),
-            keep.tile([P, S // 2], U32, name="picked1", tag="w_picked", align_bytes=64),
+            reuse.tile([P, S // 2], U32, name="picked1", offset=2048, align_bytes=64),
         )
         y = keep.tile([P, S], F32, name="y", align_bytes=64)
 
@@ -141,7 +136,11 @@ def tile_picked_lerp_none_p_kernel(
             return acc
 
         gather_words(0, 512)
-        quantise(1)
+        nc.vector.quantize_mx(
+            out=w_codes[:].bitcast(FP8X4),
+            scales=w_plane[:],
+            in_=w_bf[:].rearrange("p m j -> p (m j)"),
+        )
         for a in (0, 256):
             nc.scalar.copy(y[:, a : a + 256], project(a, a + 256)[:])
         gather_words(512, 768)

@@ -21,7 +21,7 @@ P = 128
 PACK = 4
 LANES = 16
 HEAD = 832
-SCALAR_SHARE = 40
+SCALAR_SHARE = 96
 
 
 def tile_picked_lerp_none_p_kernel(
@@ -37,8 +37,8 @@ def tile_picked_lerp_none_p_kernel(
         left_sb = keep.tile([P, V // LANES], U16, name="left_sb")
         right_sb = keep.tile([P, V // LANES], U16, name="right_sb")
         w_halves = (
-            keep.tile([P, PACK, M // 2], F32, name="w_early", align_bytes=64),
-            reuse.tile([P, PACK, M // 2], F32, name="w_late", offset=1536, align_bytes=64),
+            keep.tile([P, 2, M], F32, name="w_first", align_bytes=64),
+            reuse.tile([P, 2, M], F32, name="w_second", offset=1536, align_bytes=64),
         )
         w_hbm = w1.rearrange("(p j) m -> p j m", j=PACK)
         words = keep.tile([P, T], I32, name="words", align_bytes=64)
@@ -55,24 +55,18 @@ def tile_picked_lerp_none_p_kernel(
         words_hbm = x_words[0].rearrange("p n t -> p (n t)").bitcast(I32)
         nc.sync.dma_start(out=words[:, :HEAD], in_=words_hbm[:, :HEAD])
         nc.sync.dma_start(offs_sb[:], offs)
-        nc.sync.dma_start(out=frac_rows[P - runs :, :], in_=frac[0].rearrange("(c n) -> c n", n=P))
+        nc.scalar.dma_start(out=frac_rows[P - runs :, :], in_=frac[0].rearrange("(c n) -> c n", n=P))
         nc.sync.dma_start(left_sb[:], left)
         for a, b in scale_halves:
             nc.sync.dma_start(out=scale_rows[32:96:4, a:b].bitcast(I32), in_=x_scales[0, :, a:b].bitcast(I32))
         nc.sync.dma_start(out=words[:, HEAD:], in_=words_hbm[:, HEAD:])
-        nc.sync.dma_start(out=w_halves[0][:], in_=w_hbm[:, :, : M // 2])
-        nc.sync.dma_start(out=w_halves[1][:], in_=w_hbm[:, :, M // 2 :])
+        nc.sync.dma_start(out=w_halves[0][:], in_=w_hbm[:, :2, :])
+        nc.sync.dma_start(out=w_halves[1][:], in_=w_hbm[:, 2:, :])
         nc.sync.dma_start(right_sb[:], right)
 
         w_codes = keep.tile([P, M], U32, name="w_codes", align_bytes=64)
         w_plane = keep.tile([P, M], U8, name="w_plane", align_bytes=64)
         w_bf = keep.tile([P, M, PACK], BF16, name="w_bf", align_bytes=64)
-
-        def weave_on_scalar(h, count):
-            nc.scalar.copy(
-                w_bf[:, h * M // 2 : h * M // 2 + count, :].rearrange("p (c i) j -> p c j i", i=4),
-                w_halves[h][:, :, :count].rearrange("p j (c i) -> p c j i", i=4),
-            )
 
         picked_scales = keep.tile([P, S], U8, name="picked_scales", align_bytes=64)
         nc.vector.tensor_copy(picked_scales[:], scale_rows[:].indirect(offs_sb[:]))
@@ -96,16 +90,20 @@ def tile_picked_lerp_none_p_kernel(
                 in_=picked_scales[32 + 16 * q : 48 + 16 * q : 4, :].bitcast(I32),
             )
 
-        weave_on_scalar(0, M // 2)
-        weave_on_scalar(1, SCALAR_SHARE)
-        nc.gpsimd.tensor_scalar(
-            w_bf[:, M // 2 + SCALAR_SHARE :, :],
-            w_halves[1][:, :, SCALAR_SHARE:].rearrange("p j m -> p m j"),
-            1.0,
-            0.0,
-            MULT,
-            ADD,
-        )
+        for h in range(2):
+            nc.scalar.copy(
+                w_bf[:, :SCALAR_SHARE, 2 * h : 2 * h + 2],
+                w_halves[h][:, :, :SCALAR_SHARE].rearrange("p j m -> p m j"),
+            )
+        for h in range(2):
+            nc.gpsimd.tensor_scalar(
+                w_bf[:, SCALAR_SHARE:, 2 * h : 2 * h + 2],
+                w_halves[h][:, :, SCALAR_SHARE:].rearrange("p j m -> p m j"),
+                1.0,
+                0.0,
+                MULT,
+                ADD,
+            )
 
         rest_sb = reuse.tile([P, V], F32, name="rest_sb", offset=0, align_bytes=64)
         nc.scalar.activation(rest_sb[:], frac_bank[:], COPY, bias=1.0, scale=-1.0)

@@ -22,6 +22,7 @@ PACK = 4
 LANES = 16
 HEAD = 832
 SCALAR_SHARE = 96
+FIRST = 640
 
 
 def tile_picked_lerp_none_p_kernel(
@@ -109,16 +110,16 @@ def tile_picked_lerp_none_p_kernel(
         nc.scalar.activation(rest_sb[:], frac_bank[:], COPY, bias=1.0, scale=-1.0)
 
         picked = (
-            keep.tile([P, S // 2], U32, name="picked0", align_bytes=64),
-            reuse.tile([P, S // 2], U32, name="picked1", offset=2048, align_bytes=64),
+            keep.tile([P, FIRST], U32, name="picked0", align_bytes=64),
+            reuse.tile([P, S - FIRST], U32, name="picked1", offset=2048, align_bytes=64),
         )
         y = keep.tile([P, S], F32, name="y", align_bytes=64)
 
+        def picked_words(a, b):
+            return picked[0][:, a:b] if b <= FIRST else picked[1][:, a - FIRST : b - FIRST]
+
         def gather_words(a, b):
-            nc.vector.tensor_copy(
-                picked[a // 512][:, a % 512 : a % 512 + b - a],
-                words[:].bitcast(U32).indirect(offs_sb[:, a // LANES : b // LANES]),
-            )
+            nc.vector.tensor_copy(picked_words(a, b), words[:].bitcast(U32).indirect(offs_sb[:, a // LANES : b // LANES]))
 
         def project(a, b):
             acc = psum.tile([M, b - a], F32, name="acc%d" % a)
@@ -126,14 +127,14 @@ def tile_picked_lerp_none_p_kernel(
                 out=acc[:],
                 lhsT=w_codes[:].bitcast(FP8X4),
                 lhsT_scale=w_plane[:],
-                rhs=picked[a // 512][:, a % 512 : a % 512 + b - a].bitcast(FP8X4),
+                rhs=picked_words(a, b).bitcast(FP8X4),
                 rhs_scale=x_plane[:, a:b],
                 start=True,
                 stop=True,
             )
             return acc
 
-        gather_words(0, 512)
+        gather_words(0, FIRST)
         nc.vector.quantize_mx(
             out=w_codes[:].bitcast(FP8X4),
             scales=w_plane[:],
@@ -141,11 +142,10 @@ def tile_picked_lerp_none_p_kernel(
         )
         for a in (0, 256):
             nc.scalar.copy(y[:, a : a + 256], project(a, a + 256)[:])
-        gather_words(512, 768)
-        nc.scalar.copy(y[:, 512:768], project(512, 768)[:])
-        gather_words(768, 1024)
-        nc.vector.tensor_copy(y[:, 768:896], project(768, 896)[:])
-        nc.scalar.copy(y[:, 896:1024], project(896, 1024)[:])
+        gather_words(FIRST, S)
+        for a in range(512, S, 256):
+            nc.vector.tensor_copy(y[:, a : a + 128], project(a, a + 128)[:])
+            nc.scalar.copy(y[:, a + 128 : a + 256], project(a + 128, a + 256)[:])
 
         from_left = keep.tile([P, V], F32, name="from_left")
         at_right = keep.tile([P, V], F32, name="at_right")

@@ -159,5 +159,5 @@ def tile_picked_lerp_none_p_kernel(
             nc.vector.tensor_tensor(from_right[:, a:b], at_right[:, a:b], frac_bank[:, a:b], MULT)
         for a, b in ((0, 128), (128, 256), (256, V)):
             nc.vector.tensor_tensor(result[:, a:b], from_left[:, a:b], from_right[:, a:b], ADD)
-        for a, b in ((0, V // 2), (V // 2, V)):
+        for a, b in ((0, 128), (128, V)):
             nc.scalar.dma_start(out=out[:, a:b], in_=result[:, a:b])

@@ -21,7 +21,7 @@ P = 128
 PACK = 4
 LANES = 16
 HEAD = 832
-SCALAR_SHARE = 96
+SCALAR_SHARE = 88
 FIRST = 640
 
 
@@ -37,17 +37,12 @@ def tile_picked_lerp_none_p_kernel(
         offs_sb = keep.tile([P, S // LANES], U16, name="offs_sb")
         left_sb = keep.tile([P, V // LANES], U16, name="left_sb")
         right_sb = keep.tile([P, V // LANES], U16, name="right_sb")
-        w_halves = (
-            keep.tile([P, 2, M], F32, name="w_first", align_bytes=64),
-            reuse.tile([P, 2, M], F32, name="w_second", offset=1536, align_bytes=64),
-        )
+        w_raw = reuse.tile([P, PACK, M], F32, name="w_raw", offset=1024, align_bytes=64)
         w_hbm = w1.rearrange("(p j) m -> p j m", j=PACK)
         words = keep.tile([P, T], I32, name="words", align_bytes=64)
         scale_rows = keep.tile([P, T], U8, name="scale_rows", align_bytes=64)
 
-        scale_halves = ((0, T // 2), (T // 2, T))
-        for a, b in scale_halves:
-            nc.vector.memset(scale_rows[:, a:b].bitcast(I32), 0)
+        nc.vector.memset(scale_rows[:].bitcast(I32), 0)
         runs = V // P
         frac_rows = keep.tile([P, P], F32, name="frac_rows", tag="rows_plane", align_bytes=64)
         nc.vector.memset(frac_rows[: P - runs, :], 0.0)
@@ -57,19 +52,17 @@ def tile_picked_lerp_none_p_kernel(
         nc.sync.dma_start(out=words[:, :HEAD], in_=words_hbm[:, :HEAD])
         nc.sync.dma_start(offs_sb[:], offs)
         nc.scalar.dma_start(out=frac_rows[P - runs :, :], in_=frac[0].rearrange("(c n) -> c n", n=P))
-        nc.sync.dma_start(left_sb[:], left)
-        for a, b in scale_halves:
-            nc.sync.dma_start(out=scale_rows[32:96:4, a:b].bitcast(I32), in_=x_scales[0, :, a:b].bitcast(I32))
+        nc.sync.dma_start(out=scale_rows[32:96:4, :].bitcast(I32), in_=x_scales[0].bitcast(I32))
         nc.sync.dma_start(out=words[:, HEAD:], in_=words_hbm[:, HEAD:])
-        nc.sync.dma_start(out=w_halves[0][:], in_=w_hbm[:, :2, :])
-        nc.sync.dma_start(out=w_halves[1][:], in_=w_hbm[:, 2:, :])
+        nc.sync.dma_start(out=w_raw[:], in_=w_hbm)
         nc.sync.dma_start(right_sb[:], right)
+        nc.sync.dma_start(left_sb[:], left)
 
         w_codes = keep.tile([P, M], U32, name="w_codes", align_bytes=64)
         w_plane = keep.tile([P, M], U8, name="w_plane", align_bytes=64)
         w_bf = keep.tile([P, M, PACK], BF16, name="w_bf", align_bytes=64)
 
-        picked_scales = keep.tile([P, S], U8, name="picked_scales", align_bytes=64)
+        picked_scales = keep.tile([P, S], U8, name="picked_scales", tag="bytes_frac", align_bytes=64)
         nc.vector.tensor_copy(picked_scales[:], scale_rows[:].indirect(offs_sb[:]))
         make_identity(nc, ident[:], nomemset=True)
         turned = psum.tile([P, P], F32, name="turned")
@@ -79,32 +72,31 @@ def tile_picked_lerp_none_p_kernel(
         frac_bank = psum.tile([P, V], F32, name="frac_bank")
         for c in range(runs):
             nc.tensor.transpose(frac_bank[:, c * P : (c + 1) * P], frac_cols[:, c : c + 1].to_broadcast([P, P]), ident[:])
-        middle, last = (256, 384), (384, V)
-        frac_middle = keep.tile([P, middle[1] - middle[0]], F32, name="frac_middle", align_bytes=64)
-        nc.scalar.copy(frac_middle[:], frac_bank[:, middle[0] : middle[1]])
 
         x_plane = keep.tile([P, S], U8, name="x_plane", tag="rows_plane", align_bytes=64)
         nc.gpsimd.memset(x_plane[:].bitcast(I32), 0)
-        for q, queue in enumerate((nc.sync, nc.sync, nc.sync, nc.scalar)):
+        moves = ((nc.scalar, 3, 0, S), (nc.sync, 0, 0, S), (nc.sync, 1, 0, S), (nc.sync, 2, 0, FIRST), (nc.sync, 2, FIRST, S))
+        for queue, q, a, b in moves:
             queue.dma_start(
-                out=x_plane[32 * q : 32 * q + 4, :].bitcast(I32),
-                in_=picked_scales[32 + 16 * q : 48 + 16 * q : 4, :].bitcast(I32),
+                out=x_plane[32 * q : 32 * q + 4, a:b].bitcast(I32),
+                in_=picked_scales[32 + 16 * q : 48 + 16 * q : 4, a:b].bitcast(I32),
             )
+        middle, last = (256, 384), (384, V)
+        frac_middle = keep.tile([P, middle[1] - middle[0]], F32, name="frac_middle", tag="bytes_frac", align_bytes=64)
+        nc.sync.dma_start(out=frac_middle[:], in_=frac[:, middle[0] : middle[1]])
 
-        for h in range(2):
-            nc.scalar.copy(
-                w_bf[:, :SCALAR_SHARE, 2 * h : 2 * h + 2],
-                w_halves[h][:, :, :SCALAR_SHARE].rearrange("p j m -> p m j"),
-            )
-        for h in range(2):
-            nc.gpsimd.tensor_scalar(
-                w_bf[:, SCALAR_SHARE:, 2 * h : 2 * h + 2],
-                w_halves[h][:, :, SCALAR_SHARE:].rearrange("p j m -> p m j"),
-                1.0,
-                0.0,
-                MULT,
-                ADD,
-            )
+        nc.scalar.copy(
+            w_bf[:, :SCALAR_SHARE, :].rearrange("p (c i) j -> p c j i", i=4),
+            w_raw[:, :, :SCALAR_SHARE].rearrange("p j (c i) -> p c j i", i=4),
+        )
+        nc.gpsimd.tensor_scalar(
+            w_bf[:, SCALAR_SHARE:, :],
+            w_raw[:, :, SCALAR_SHARE:].rearrange("p j m -> p m j"),
+            1.0,
+            0.0,
+            MULT,
+            ADD,
+        )
 
         rest_sb = reuse.tile([P, V], F32, name="rest_sb", offset=0, align_bytes=64)
         nc.scalar.activation(rest_sb[:], frac_bank[:], COPY, bias=1.0, scale=-1.0)

@@ -37,10 +37,10 @@ def tile_picked_lerp_none_p_kernel(
         offs_sb = keep.tile([P, S // LANES], U16, name="offs_sb")
         left_sb = keep.tile([P, V // LANES], U16, name="left_sb")
         right_sb = keep.tile([P, V // LANES], U16, name="right_sb")
-        w_raw = reuse.tile([P, PACK, M], F32, name="w_raw", offset=1024, align_bytes=64)
+        w_raw = reuse.tile([P, PACK, M], F32, name="w_raw", offset=1024, align_bytes=256)
         w_hbm = w1.rearrange("(p j) m -> p j m", j=PACK)
-        words = keep.tile([P, T], I32, name="words", align_bytes=64)
-        scale_rows = keep.tile([P, T], U8, name="scale_rows", align_bytes=64)
+        words = keep.tile([P, T], I32, name="words", align_bytes=256)
+        scale_rows = keep.tile([P, T], U8, name="scale_rows", align_bytes=256)
 
         nc.vector.memset(scale_rows[:].bitcast(I32), 0)
         runs = V // P
@@ -98,12 +98,12 @@ def tile_picked_lerp_none_p_kernel(
             ADD,
         )
 
-        rest_sb = reuse.tile([P, V], F32, name="rest_sb", offset=0, align_bytes=64)
+        rest_sb = reuse.tile([P, V], F32, name="rest_sb", offset=0, align_bytes=256)
         nc.scalar.activation(rest_sb[:], frac_bank[:], COPY, bias=1.0, scale=-1.0)
 
         picked = (
             keep.tile([P, FIRST], U32, name="picked0", align_bytes=64),
-            reuse.tile([P, S - FIRST], U32, name="picked1", offset=2048, align_bytes=64),
+            reuse.tile([P, S - FIRST], U32, name="picked1", offset=2048, align_bytes=256),
         )
         y = keep.tile([P, S], F32, name="y", align_bytes=64)
 
@@ -142,7 +142,7 @@ def tile_picked_lerp_none_p_kernel(
         from_left = keep.tile([P, V], F32, name="from_left")
         at_right = keep.tile([P, V], F32, name="at_right")
         from_right = keep.tile([P, V], F32, name="from_right")
-        result = keep.tile([P, V], F32, name="result")
+        result = keep.tile([P, V], F32, name="result", align_bytes=256)
         for a, b in ((0, last[0]), last):
             nc.scalar.activation(at_right[:, a:b], y[:].indirect(right_sb[:, a // LANES : b // LANES]), COPY)
         nc.vector.tensor_tensor(from_left[:], y[:].indirect(left_sb[:]), rest_sb[:], MULT)

@@ -75,7 +75,7 @@ def tile_picked_lerp_none_p_kernel(
 
         x_plane = keep.tile([P, S], U8, name="x_plane", tag="rows_plane", align_bytes=64)
         nc.gpsimd.memset(x_plane[:].bitcast(I32), 0)
-        moves = ((nc.scalar, 3, 0, S), (nc.sync, 0, 0, S), (nc.sync, 1, 0, S), (nc.sync, 2, 0, FIRST), (nc.sync, 2, FIRST, S))
+        moves = ((nc.scalar, 3, 0, S), (nc.sync, 0, 0, S), (nc.scalar, 1, 0, S), (nc.sync, 2, 0, FIRST), (nc.sync, 2, FIRST, S))
         for queue, q, a, b in moves:
             queue.dma_start(
                 out=x_plane[32 * q : 32 * q + 4, a:b].bitcast(I32),

@@ -81,7 +81,7 @@ def tile_picked_lerp_none_p_kernel(
                 out=x_plane[32 * q : 32 * q + 4, a:b].bitcast(I32),
                 in_=picked_scales[32 + 16 * q : 48 + 16 * q : 4, a:b].bitcast(I32),
             )
-        middle, last = (256, 384), (384, V)
+        middle, last = (192, 320), (320, V)
         frac_middle = keep.tile([P, middle[1] - middle[0]], F32, name="frac_middle", tag="bytes_frac", align_bytes=64)
         nc.sync.dma_start(out=frac_middle[:], in_=frac[:, middle[0] : middle[1]])
 
@@ -147,9 +147,9 @@ def tile_picked_lerp_none_p_kernel(
             nc.scalar.activation(at_right[:, a:b], y[:].indirect(right_sb[:, a // LANES : b // LANES]), COPY)
         nc.vector.tensor_tensor(from_left[:], y[:].indirect(left_sb[:]), rest_sb[:], MULT)
         nc.gpsimd.tensor_tensor(from_right[:, middle[0] : middle[1]], at_right[:, middle[0] : middle[1]], frac_middle[:], MULT)
-        for a, b in ((0, 128), (128, 256), last):
+        for a, b in ((0, 192), last):
             nc.vector.tensor_tensor(from_right[:, a:b], at_right[:, a:b], frac_bank[:, a:b], MULT)
-        for a, b in ((0, 128), (128, 256), (256, V)):
+        for a, b in ((0, 192), middle, last):
             nc.vector.tensor_tensor(result[:, a:b], from_left[:, a:b], from_right[:, a:b], ADD)
-        for a, b in ((0, 128), (128, V)):
+        for a, b in ((0, 192), (192, V)):
             nc.scalar.dma_start(out=out[:, a:b], in_=result[:, a:b])

@@ -20,7 +20,7 @@ COPY = mybir.ActivationFunctionType.Copy
 P = 128
 PACK = 4
 LANES = 16
-HEAD = 832
+HEAD = 1024
 SCALAR_SHARE = 88
 FIRST = 640
 

from contextlib import ExitStack

import concourse.mybir as mybir
from concourse.masks import make_identity

K, T, S, V, M = 512, 4096, 1024, 512, 128
FLOPS = 2 * K * M * S

F32 = mybir.dt.float32
BF16 = mybir.dt.bfloat16
I32 = mybir.dt.int32
U32 = mybir.dt.uint32
U16 = mybir.dt.uint16
U8 = mybir.dt.uint8
FP8X4 = mybir.dt.float8_e4m3fn_x4
MULT = mybir.AluOpType.mult
ADD = mybir.AluOpType.add
COPY = mybir.ActivationFunctionType.Copy

P = 128
PACK = 4
LANES = 16
HEAD = 1024
SCALAR_SHARE = 88
FIRST = 640


def tile_picked_lerp_none_p_kernel(
    tc, x_words, x_scales, w1, frac, offs, left, right, out
):
    nc = tc.nc
    with ExitStack() as ctx:
        keep = ctx.enter_context(tc.tile_pool(name="keep", bufs=1))
        reuse = ctx.enter_context(tc.tile_pool(name="reuse", bufs=1))
        psum = ctx.enter_context(tc.psum_pool(name="psum", bufs=1))

        offs_sb = keep.tile([P, S // LANES], U16, name="offs_sb")
        left_sb = keep.tile([P, V // LANES], U16, name="left_sb")
        right_sb = keep.tile([P, V // LANES], U16, name="right_sb")
        w_raw = reuse.tile([P, PACK, M], F32, name="w_raw", offset=1024, align_bytes=256)
        w_hbm = w1.rearrange("(p j) m -> p j m", j=PACK)
        words = keep.tile([P, T], I32, name="words", align_bytes=256)
        scale_rows = keep.tile([P, T], U8, name="scale_rows", align_bytes=256)

        nc.vector.memset(scale_rows[:].bitcast(I32), 0)
        runs = V // P
        frac_rows = keep.tile([P, P], F32, name="frac_rows", tag="rows_plane", align_bytes=64)
        nc.vector.memset(frac_rows[: P - runs, :], 0.0)
        ident = keep.tile([P, P], F32, name="ident")
        nc.vector.memset(ident[:], 0.0)
        words_hbm = x_words[0].rearrange("p n t -> p (n t)").bitcast(I32)
        nc.sync.dma_start(out=words[:, :HEAD], in_=words_hbm[:, :HEAD])
        nc.sync.dma_start(offs_sb[:], offs)
        nc.scalar.dma_start(out=frac_rows[P - runs :, :], in_=frac[0].rearrange("(c n) -> c n", n=P))
        nc.sync.dma_start(out=scale_rows[32:96:4, :].bitcast(I32), in_=x_scales[0].bitcast(I32))
        nc.sync.dma_start(out=words[:, HEAD:], in_=words_hbm[:, HEAD:])
        nc.sync.dma_start(out=w_raw[:], in_=w_hbm)
        nc.sync.dma_start(right_sb[:], right)
        nc.sync.dma_start(left_sb[:], left)

        w_codes = keep.tile([P, M], U32, name="w_codes", align_bytes=64)
        w_plane = keep.tile([P, M], U8, name="w_plane", align_bytes=64)
        w_bf = keep.tile([P, M, PACK], BF16, name="w_bf", align_bytes=64)

        picked_scales = keep.tile([P, S], U8, name="picked_scales", tag="bytes_frac", align_bytes=64)
        nc.vector.tensor_copy(picked_scales[:], scale_rows[:].indirect(offs_sb[:]))
        make_identity(nc, ident[:], nomemset=True)
        turned = psum.tile([P, P], F32, name="turned")
        nc.tensor.transpose(turned[:], frac_rows[:], ident[:])
        frac_cols = keep.tile([P, runs], F32, name="frac_cols")
        nc.scalar.copy(frac_cols[:], turned[:, P - runs :])
        frac_bank = psum.tile([P, V], F32, name="frac_bank")
        for c in range(runs):
            nc.tensor.transpose(frac_bank[:, c * P : (c + 1) * P], frac_cols[:, c : c + 1].to_broadcast([P, P]), ident[:])

        x_plane = keep.tile([P, S], U8, name="x_plane", tag="rows_plane", align_bytes=64)
        nc.gpsimd.memset(x_plane[:].bitcast(I32), 0)
        moves = ((nc.scalar, 3, 0, S), (nc.sync, 0, 0, S), (nc.scalar, 1, 0, S), (nc.sync, 2, 0, FIRST), (nc.sync, 2, FIRST, S))
        for queue, q, a, b in moves:
            queue.dma_start(
                out=x_plane[32 * q : 32 * q + 4, a:b].bitcast(I32),
                in_=picked_scales[32 + 16 * q : 48 + 16 * q : 4, a:b].bitcast(I32),
            )
        middle, last = (192, 320), (320, V)
        frac_middle = keep.tile([P, middle[1] - middle[0]], F32, name="frac_middle", tag="bytes_frac", align_bytes=64)
        nc.sync.dma_start(out=frac_middle[:], in_=frac[:, middle[0] : middle[1]])

        nc.scalar.copy(
            w_bf[:, :SCALAR_SHARE, :].rearrange("p (c i) j -> p c j i", i=4),
            w_raw[:, :, :SCALAR_SHARE].rearrange("p j (c i) -> p c j i", i=4),
        )
        nc.gpsimd.tensor_scalar(
            w_bf[:, SCALAR_SHARE:, :],
            w_raw[:, :, SCALAR_SHARE:].rearrange("p j m -> p m j"),
            1.0,
            0.0,
            MULT,
            ADD,
        )

        rest_sb = reuse.tile([P, V], F32, name="rest_sb", offset=0, align_bytes=256)
        nc.scalar.activation(rest_sb[:], frac_bank[:], COPY, bias=1.0, scale=-1.0)

        picked = (
            keep.tile([P, FIRST], U32, name="picked0", align_bytes=64),
            reuse.tile([P, S - FIRST], U32, name="picked1", offset=2048, align_bytes=256),
        )
        y = keep.tile([P, S], F32, name="y", align_bytes=64)

        def picked_words(a, b):
            return picked[0][:, a:b] if b <= FIRST else picked[1][:, a - FIRST : b - FIRST]

        def gather_words(a, b):
            nc.vector.tensor_copy(picked_words(a, b), words[:].bitcast(U32).indirect(offs_sb[:, a // LANES : b // LANES]))

        def project(a, b):
            acc = psum.tile([M, b - a], F32, name="acc%d" % a)
            nc.tensor.matmul_mx(
                out=acc[:],
                lhsT=w_codes[:].bitcast(FP8X4),
                lhsT_scale=w_plane[:],
                rhs=picked_words(a, b).bitcast(FP8X4),
                rhs_scale=x_plane[:, a:b],
                start=True,
                stop=True,
            )
            return acc

        gather_words(0, FIRST)
        nc.vector.quantize_mx(
            out=w_codes[:].bitcast(FP8X4),
            scales=w_plane[:],
            in_=w_bf[:].rearrange("p m j -> p (m j)"),
        )
        for a in (0, 256):
            nc.scalar.copy(y[:, a : a + 256], project(a, a + 256)[:])
        gather_words(FIRST, S)
        for a in range(512, S, 256):
            nc.vector.tensor_copy(y[:, a : a + 128], project(a, a + 128)[:])
            nc.scalar.copy(y[:, a + 128 : a + 256], project(a + 128, a + 256)[:])

        from_left = keep.tile([P, V], F32, name="from_left")
        at_right = keep.tile([P, V], F32, name="at_right")
        from_right = keep.tile([P, V], F32, name="from_right")
        result = keep.tile([P, V], F32, name="result", align_bytes=256)
        for a, b in ((0, last[0]), last):
            nc.scalar.activation(at_right[:, a:b], y[:].indirect(right_sb[:, a // LANES : b // LANES]), COPY)
        nc.vector.tensor_tensor(from_left[:], y[:].indirect(left_sb[:]), rest_sb[:], MULT)
        nc.gpsimd.tensor_tensor(from_right[:, middle[0] : middle[1]], at_right[:, middle[0] : middle[1]], frac_middle[:], MULT)
        for a, b in ((0, 192), last):
            nc.vector.tensor_tensor(from_right[:, a:b], at_right[:, a:b], frac_bank[:, a:b], MULT)
        for a, b in ((0, 192), middle, last):
            nc.vector.tensor_tensor(result[:, a:b], from_left[:, a:b], from_right[:, a:b], ADD)
        for a, b in ((0, 192), (192, V)):
            nc.scalar.dma_start(out=out[:, a:b], in_=result[:, a:b])
